import numpy as np, ml_dtypes
CORES = [1,5,17,21,33,37,49,53]
N = 8
import mx_ref
BF = ml_dtypes.bfloat16
def gcols(t, e):
    v = np.concatenate([t.reshape(8, 16, -1, 4), np.zeros((8, 16, 1, 4), BF)], axis=2)
    return np.ascontiguousarray(np.stack([v[g][:, e[g]] for g in range(8)])).reshape(128, -1)
def tile(rs):
    return np.stack(rs, axis=2).reshape(128, -1).astype(BF)
def pick(q, e):
    c = np.concatenate([q[0].reshape(128, -1, 4), np.zeros((128, 1, 4), np.uint8)], axis=1); s = np.concatenate([q[1], np.ones((16, 1), np.uint8)], axis=1)
    return (np.ascontiguousarray(c[:, e].reshape(128, -1)), np.ascontiguousarray(s[:, e]))
def join(*qs):
    return (np.concatenate([q[0] for q in qs], axis=1), np.concatenate([q[1] for q in qs], axis=1))
def put(q, e, v):
    c, s = q[0].reshape(128, -1, 4).copy(), q[1].copy(); c[:, e] = v[0].reshape(128, -1, 4); s[:, e] = v[1]
    return (c.reshape(128, -1), s)
def pk(c, s):
    return (np.ascontiguousarray(c), mx_ref.live(s))
def emit(q):
    return q[0], q[1]
def packed(v, rng):
    q = [mx_ref.quantize(np.ascontiguousarray(v[r])) for r in range(N)]
    return np.stack([a for a, b in q]), np.stack([mx_ref.plane(b, rng) for a, b in q])
def values_of_codes():
    e, c = np.zeros((128, 128, 4), np.float32), np.zeros((128, 2, 4), np.uint8)
    e[np.arange(128), np.arange(128), 0] = 1
    c[:127, :, 0] = np.arange(256).reshape(2, 128).T[:127]
    return mx_ref.matmul(mx_ref.quantize(e.reshape(128, 512).astype(BF)), (c.reshape(128, 8), np.full((16, 2), 127, np.uint8))).T.reshape(-1).astype(np.float64)
CODE_VALUE, SCALE_VALUE = values_of_codes(), 2.0 ** (np.arange(256) - 127.0)
def decode(q):
    return (CODE_VALUE[q[0]].reshape(16, 8, -1, 4) * SCALE_VALUE[q[1]][:, None, :, None] + 0.0).reshape(128, -1).astype(np.float32)
def f(rng, *shape):
    return mx_ref.flush((rng.standard_normal(shape, dtype=np.float32) * np.exp2(rng.integers(-2, 3, shape[:-1] + (1,)))).astype(BF))
def wide(rng, *shape, cols=0):
    v = rng.standard_normal(shape, dtype=np.float32) * np.exp2(rng.integers(-12, 13, shape)).astype(np.float32)
    if cols: v *= np.repeat(np.exp2(rng.integers(-cols, cols + 1, shape[:-2] + (1, shape[-1] // 4))) * (rng.random(shape[:-2] + (1, shape[-1] // 4)) > 0.0625), 4, axis=-1).astype(np.float32)
    return mx_ref.flush(v.astype(BF))
C, K, DEP, R = 256, 128, 32, 3
SOURCE = [7, 0, 1, 1, 2, 2, 3, 3]
LEVEL = [0, 1, 2, 2, 3, 3, 3, 3]
ITEM = 8 * (np.arange(C) % DEP) + np.arange(C) // DEP
def big(v):
    v = v.astype(np.float32)
    v[np.abs(v) < np.float32(2.0 ** -16)] = 0
    return v.astype(BF)
def numbers_of(rng):
    return {"x": big(f(rng, N, 128, 4 * C)), "u": np.array(f(rng, N, 128, 512)), "v": np.array(f(rng, N, 128, 512))}
def layers(rng):
    return big(f(rng, N, 128, 2048).astype(np.float32) * np.float32(0.5)).reshape(N, 8, 16, 4, 8, 16, 4)
def weights(rng, w):
    c, p = packed(np.ascontiguousarray(w).reshape(N, 128, 2048), rng)
    return {"wc": c, "ws": p}
def own_bits(u):
    for b in range(3): u[:, :, b::16] = 0
    for h in range(0, 128, 16):
        for b in range(3): u[:, h, h + b, b] = 1
def setup_inputs(rng):
    return {**numbers_of(rng), **weights(rng, layers(rng))}
def setup_inputs_ties(rng):
    d = numbers_of(rng)
    e = rng.permutation(N)
    k = rng.integers(-1, 2, (N, 8, C, 3)).astype(np.float32)
    k[e[0]] = 0
    k[e[1]] = 1
    for g in range(8): k[e[2], g, :, 0] = 2.0 * (LEVEL[g] % 2) - 1.0
    x = d["x"].reshape(N, 8, 16, C, 4)
    x[:, :, :8] = 0
    x[:, :, 0, :, :3] = k.astype(BF)
    u = d["u"].reshape(N, 128, 128, 4)
    own_bits(u)
    w = layers(rng)
    w[:, :, :, :, :, :8] = 0
    return {"x": x.reshape(N, 128, 4 * C), "u": u.reshape(N, 128, 512), "v": d["v"], **weights(rng, w)}
def setup_inputs_near(rng):
    d = numbers_of(rng)
    x = d["x"].reshape(N, 8, 16, C, 4)
    u = d["u"].reshape(N, 128, 128, 4)
    o = rng.permutation(N) % 4
    x[:, :, :8] = 0
    for b in range(3): u[:, :, b::16] = 0
    for r in range(N):
        a = rng.integers(-1, 2, (8, C, 3)).astype(np.float32)
        b = np.where(rng.random((8, C, 3)) < 0.75, -a, rng.integers(-1, 2, (8, C, 3))).astype(np.float32)
        k = np.float32(2.0 ** -27 if o[r] < 2 else 1.0)
        a, b = a * k, b * k
        for g in rng.permutation(8)[:4]: a[g, rng.integers(C)] = 2.0 ** 18 * rng.choice([-1.0, 1.0], 3)
        x[r, :, 0, :, :3] = a.astype(BF)
        x[r, :, 1, :, :3] = b.astype(BF)
        m = 2.0 ** -30 if o[r] % 2 == 0 else 1.0
        for h in range(0, 128, 16):
            for t in range(3):
                u[r, h, h + t, t] = 1.125 * m
                u[r, h + 1, h + t, t] = m
    w = layers(rng)
    w[:, :, :8] = 0
    w[:, :, :, :, :, :8] = 0
    return {"x": x.reshape(N, 128, 4 * C), "u": u.reshape(N, 128, 512), "v": d["v"], **weights(rng, w)}
def setup_inputs_late(rng):
    d = numbers_of(rng)
    s = rng.integers(6, 8, (N, 8, 8, DEP))
    for g in range(8):
        if g: s[:, g, :, 0] = LEVEL[g] - 1
        s[:, g, :, -1] = LEVEL[g]
    s[:, 7, 7] = 0
    s[:, 7, 7, -1] = 2
    e = int(rng.integers(N))
    s[e] = 7
    for g in range(8):
        if LEVEL[g] > 0: s[e, g, :, 0] = 7 - LEVEL[g]
        if LEVEL[g] < 3: s[e, g, :, -1] = 6 - LEVEL[g]
    s[e, 2:4, :7, -1] = 2
    for h in (0, 1, 6, 7):
        s[e, 4:, h, 0] = 2
        s[e, 4:, h, 1] = 3
    s[e, 4:, 5, 1] = 6
    s = s.reshape(N, 8, C)
    x = d["x"].reshape(N, 8, 16, C, 4)
    x[:, :, :8] = 0
    x[:, :, 0, :, :3] = (2.0 * ((s[..., None] >> np.array([2, 1, 0])) & 1) - 1.0).astype(np.float32).astype(BF)
    k = (1.0 + (2 * rng.integers(0, 64, (N, 8, 8, C, 4)) + 1) / 128.0) * np.exp2(-1.0 * rng.integers(8, 15, (N, 8, 8, C, 4))) * rng.choice([-1.0, 1.0], (N, 8, 8, C, 4))
    k[:, :, 0, :, 0] = 1.96875
    x[:, :, 8:] = k.astype(np.float32).astype(BF)
    u = d["u"].reshape(N, 128, 128, 4)
    own_bits(u)
    w = layers(rng)
    w[:, :, :, :, :, :8] = 0
    return {"x": x.reshape(N, 128, 4 * C), "u": u.reshape(N, 128, 512), "v": d["v"], **weights(rng, w)}
def setup_inputs_ends(rng):
    o = rng.permutation(N)
    x = rng.choice([-1.0, 1.0], (N, 8, 1, C, 1)) * np.ones((1, 1, 16, 1, 4))
    u, v = rng.choice([-1.0, 1.0], (N, 128, 512)), rng.choice([-1.0, 1.0], (N, 128, 512))
    w = np.zeros((N, 128, 2048), np.float32)
    for r in range(N):
        if o[r] == 0: x[r] = 1.0
        if o[r] == 3: x[r] = -1.0
        if o[r] in (0, 3): u[r] = 1.0
        x[r] *= 2.0 ** 19 if o[r] % 2 == 0 else 2.0 ** -27
        u[r] *= 2.0 ** 30 if o[r] % 4 < 2 else 2.0 ** -30
        v[r] *= 2.0 ** 30 if o[r] % 4 in (0, 3) else 2.0 ** -30
        w[r] = (2.0, -2.0, 0.0)[o[r] % 3]
    return {"x": x.astype(np.float32).reshape(N, 128, 4 * C).astype(BF), "u": u.astype(np.float32).astype(BF), "v": v.astype(np.float32).astype(BF), **weights(rng, w.astype(BF))}
def setup_inputs_spread(rng):
    d = setup_inputs(rng)
    d["x"] = big(wide(rng, N, 128, 4 * C, cols=3))
    return d
def check_inputs(d):
    b = []
    for k, m in (("x", 2.0 ** 19), ("u", 2.0 ** 30), ("v", 2.0 ** 30)):
        a = np.abs(d[k].astype(np.float32))
        if not (np.isfinite(a).all() and ((a == 0) | (a >= 2.0 ** -30) & (a <= m)).all()): b.append("a value of " + k)
    none, least, most = [emit(mx_ref.quantize(np.full((128, 16), k, np.float32).astype(BF)))[1][0, 0] for k in (0.0, 2.0 ** -30, 2.0 ** 30)]
    for r in range(N):
        if ((d["wc"][r] == 0x7F) | (d["wc"][r] == 0xFF)).any(): b.append("wc: a code that is no number")
        s = mx_ref.live(d["ws"][r])
        if ((s != none) & ((s < least) | (s > most))).any(): b.append("ws: a scale out of range")
        a = np.abs(decode(pk(d["wc"][r], d["ws"][r])).astype(np.float64)).reshape(128, 512, 4)
        if not (np.sum(a, axis=(0, 2)) <= 1024).all(): b.append("W: a column that adds up to more than 1024")
    return b
def times(sym, wait):
    sym, wait = sym.reshape(8, DEP), wait.reshape(8, DEP)
    t, last = np.zeros((8, DEP), np.int64), np.zeros(8, np.int64)
    for i in range(DEP):
        last = np.maximum(last, wait[:, i]) + (1 + sym[:, i])
        t[:, i] = last
    return t.reshape(C)
def orders(sym):
    o, b = np.zeros((8, C), np.int64), np.zeros((8, K), np.int64)
    first, least = np.full((8, 8), -1), np.zeros((8, 8), np.int64)
    for g in range(8):
        e = SOURCE[g]
        t = times(sym[g], least[e][sym[g]] if g > 0 else np.zeros(C, np.int64))
        o[g] = np.argsort(t, kind="stable")
        for s in range(8):
            p = np.flatnonzero(sym[g][o[g]] == s)
            if len(p) > 0:
                first[g, s] = o[g, p[0]]
                least[g, s] = t[o[g, p[0]]]
        l = o[g, :K]
        p = first[e][sym[g][l]] if g > 0 else l
        b[g] = np.where(p < 0, l, p)
    return o, b
def reference(x, u, v, wc, ws):
    qu = [mx_ref.quantize(u[r]) for r in range(N)]
    lay = [pk(wc[r], ws[r]) for r in range(N)]
    now = [x[r] for r in range(N)]
    order = np.zeros((N, 8, C), np.int64)
    for t in range(R):
        stay, sent = [], []
        for r in range(N):
            q = mx_ref.quantize(now[r])
            full = decode(q)
            s = mx_ref.matmul(qu[r], q)
            order[r], mate = orders(4 * (s[::16] > 0) + 2 * (s[1::16] > 0) + (s[2::16] > 0))
            a = full.reshape(8, 16, C, 4)
            z = np.stack([(a[g][:, order[r, g, :K]] + a[SOURCE[g]][:, mate[g]]) * np.float32(0.5) for g in range(8)])
            sent.append(mx_ref.quantize(np.ascontiguousarray(z.reshape(128, 4 * K).astype(BF))))
            stay.append(gcols(full.astype(BF), order[r][:, K:]))
        for r in range(N):
            q = sent[r - 1]
            d = decode(q)
            h = tile([mx_ref.matmul(pick(lay[r], np.arange(128 * b, 128 * b + 128)), q) * np.float32(0.0078125) + d[:, b::4] for b in range(4)])
            items = np.concatenate([stay[r], h], axis=1).reshape(128, C, 4)
            now[r] = np.ascontiguousarray(items[:, ITEM].reshape(128, 4 * C))
    y, op = np.zeros((N, 128, C), np.float32), np.zeros((N, 8, C), np.float32)
    oc, osc = np.zeros((N, 128, 4 * C), np.uint8), np.zeros((N, 16, C), np.uint8)
    for r in range(N):
        q = mx_ref.quantize(now[r])
        y[r] = mx_ref.matmul(mx_ref.quantize(v[r]), q)
        op[r] = order[r]
        oc[r], osc[r] = emit(q)
    return {"y": y, "op": op, "oc": oc, "osc": osc}

@@ -1,0 +1,467 @@
+import math
+from concourse.mybir import dt, AluOpType as A, AxisListType, ActivationFunctionType as AF
+
+NR = 3
+VUNITS = 4
+BIG = 1 << 20
+TMASK = 0x7FF00
+INTS = ["oi", "oj", "ok1", "ni", "nj", "nk", "fi", "pf", "pg", "ri", "rx"]
+FLTS = ["s1", "sn", "inv", "dif", "own", "ph", "pq", "ka", "kb", "ry", "rz", "of", "srf", "kn"]
+
+SCRATCH = {}
+
+
+def _b(name, n, d="float32"):
+    SCRATCH[name] = ("sbuf", [128, n], d)
+
+
+for _n, _k, _d in (
+        ("xs", 1024, "bfloat16"), ("us", 512, "bfloat16"), ("vs", 512, "bfloat16"),
+        ("one", 128, "bfloat16"), ("zer", 528, "bfloat16"), ("dy", 128, "bfloat16"), ("dy0", 128, "bfloat16"), ("dy1", 128, "bfloat16"),
+        ("dya", 128, "bfloat16"), ("dyb", 128, "bfloat16"), ("dyc", 128, "bfloat16"),
+        ("idn", 128, "bfloat16"), ("prm", 128, "bfloat16"),
+        ("cl", 2560, "bfloat16"), ("ce", 528, "bfloat16"), ("cg", 528, "bfloat16"),
+        ("pI", 1, "int32"), ("pi8", 1, "int32"), ("pi4", 1, "int32"), ("pi16", 1, "int32"), ("pih", 1, "int32"),
+        ("mk", 4, "float32"), ("cm", 2, "float32"), ("c8", 2, "float32"), ("cf", 8, "float32"),
+        ("io8", 8, "float32"), ("dT", 16, "float32"), ("pen", 8, "float32"), ("pwf", 8, "float32"), ("pow", 8, "int32"),
+        ("bp", 128, "float32"), ("br", 256, "float32"),
+        ("ti", 256, "int32"), ("tj", 256, "int32"), ("vrow", 256, "bfloat16"), ("vcol", 256, "float32"),
+        ("ol", 16, "uint16"), ("nl", 16, "uint16"),
+        ("sb", 48, "float32"), ("mt", 512, "bfloat16"),
+        ("l0", 8, "uint16"), ("l1", 8, "uint16"), ("l2", 8, "uint16"), ("lr", 16, "uint16"),
+        ("da", 128, "float32"), ("db", 128, "float32"), ("dc", 128, "float32"), ("dr", 256, "float32"),
+        ("wp", 128, "float32"), ("wr", 256, "float32"), ("tp", 128, "float32"), ("mm", 128, "float32"), ("mv", 1, "float32"),
+        ("rep", 32, "float32"), ("trp", 32, "float32"), ("tab0", 16, "int32"), ("tab1", 16, "int32"), ("tabr", 16, "int32"),
+        ("wt", 8, "int32"), ("wtr", 16, "int32"), ("tin", 32, "float32"), ("tout", 32, "float32"),
+        ("fl", 2, "uint16"), ("prs", 8, "float32"), ("prw", 8, "float32"), ("bb", 1, "float32"), ("gl", 16, "uint16"),
+        ("key", 272, "float32"), ("kt", 512, "float32"), ("acc", 16, "float32"), ("acr", 16, "float32"),
+        ("pl", 16, "uint16"), ("rl", 16, "uint16"),
+        ("win", 512, "bfloat16"), ("wtt", 512, "bfloat16"), ("ou", 16, "uint16"), ("opw", 256, "float32"),
+        ("F", 1024, "bfloat16"), ("G", 1088, "bfloat16"), ("Gp", 1024, "bfloat16"), ("gz", 512, "bfloat16"), ("Z", 512, "bfloat16"),
+        ("X", 1024, "bfloat16"), ("hr", 512, "float32"), ("ysb", 256, "float32")):
+    _b(_n, _k, _d)
+_b("js", 256 * (16 - VUNITS), "bfloat16")
+for _k in range(VUNITS):
+    _b("jv%d" % _k, 256, "bfloat16")
+_b("ints", 16 * len(INTS), "int32")
+_b("flts", 16 * len(FLTS), "float32")
+for _n, _k in (("qx", 256), ("qn", 1024), ("qp", 1024), ("qu", 128), ("qv", 128), ("qw", 512), ("qc", 1664), ("qm", 128),
+               ("qz", 128 * NR), ("qa", 128 * NR)):
+    _b(_n, _k, "float8_e4m3fn_x4")
+    _b("s" + _n, _k, "uint8")
+for _k in range(8):
+    SCRATCH["ps%d" % _k] = ("psum", [128, 512], "float32")
+SEMAPHORES = ["cV", "cS", "cT", "cG", "sent"] + ["arr%d" % k for k in range(NR)] + ["ld%d" % k for k in range(16)]
+
+
+def recorder(g, T):
+    eng = {"V": g.vector, "S": g.scalar, "T": g.tensor, "G": g, "Y": g.sync}
+    count = {"V": 0, "S": 0, "T": 0, "G": 0}
+    known = {q: {} for q in eng}
+    writer, readers = {}, {}
+    nd = [0]
+
+    def need(q, toks):
+        todo = {}
+        for (sem, val, own, snap) in toks:
+            if known[q].get(sem, 0) < val and todo.get(sem, (0, None))[0] < val:
+                todo[sem] = (val, snap)
+        for sem in list(todo):
+            if any(s != sem and todo[s][1].get(sem, 0) >= todo[sem][0] for s in todo):
+                continue
+            eng[q].wait_ge(T.sem[sem], todo[sem][0])
+        for sem, (val, snap) in todo.items():
+            for k, v in list(snap.items()) + [(sem, val)]:
+                if known[q].get(k, 0) < v:
+                    known[q][k] = v
+
+    def toks_of(q, reads, writes):
+        t = []
+        for r in reads:
+            if r in writer:
+                t.append(writer[r])
+            if r[:2] == "ps":
+                t += [x for x in readers.get(r, []) if x[2] != q]
+        for w in writes:
+            t += readers.get(w, [])
+            if w in writer and (writer[w][2] != q or readers.get(w)):
+                t.append(writer[w])
+        return t
+
+    def note(tok, reads, writes):
+        for w in writes:
+            writer[w] = tok
+            readers[w] = []
+        for r in reads:
+            if r not in writes:
+                readers.setdefault(r, []).append(tok)
+
+    def emit(q, make, reads, writes, dma=False):
+        need(q, toks_of(q, reads, writes))
+        ins = make()
+        if dma:
+            sem = "ld%d" % nd[0]
+            nd[0] += 1
+            ins.then_inc(T.sem[sem], 16)
+            tok = (sem, 16, "D" + sem, dict(known[q]))
+        else:
+            sem = "c" + q
+            count[q] += 1
+            ins.then_inc(T.sem[sem], 1)
+            tok = (sem, count[q], q, dict(known[q]))
+        note(tok, reads, writes)
+        return tok
+
+    def landed(sem, val, writes):
+        note((sem, val, "R" + sem, {}), [], writes)
+
+    return emit, need, toks_of, landed, count, nd
+
+
+def rank_program(g, core, T, topo):
+    rank = T.rank_of(core)
+    if rank is None:
+        return
+    nxt = T.cores[(rank + 1) % len(T.cores)]
+    prv = T.cores[(rank - 1) % len(T.cores)]
+    emit, need, toks_of, landed, count, nd = recorder(g, T)
+    v, s = g.vector, g.scalar
+
+    def I(n):
+        k = 16 * INTS.index(n)
+        return T.ints[:, k:k + 16]
+
+    def W(n, p0=0, p1=128, a=0, b=16):
+        k = 16 * FLTS.index(n)
+        return T.flts[p0:p1, k + a:k + b]
+
+    place = {"qcl": ("qc", 0), "qcr": ("qc", 384), "qce": ("qc", 640), "qcg": ("qc", 1152)}
+    for k in range(NR + 1):
+        place["qn%d" % k] = ("qn", 256 * k)
+        place["qp%d" % k] = ("qp", 256 * k)
+        place["qz%d" % k] = ("qz", 128 * k)
+        place["qa%d" % k] = ("qa", 128 * k)
+
+    def K(n, a, b):
+        q, o = place.get(n, (n, 0))
+        return T[q][:, o + a:o + b], T["s" + q][:, o + a:o + b]
+
+    def pt(n):
+        return n if isinstance(n, (list, tuple)) else [n]
+
+    def TS(o, ok, i, ik, s1, s2, o0, o1=None):
+        if o1 is None:
+            return emit("V", lambda: v.tensor_scalar(o, i, s1, None, o0), pt(ik), pt(ok))
+        return emit("V", lambda: v.tensor_scalar(o, i, s1, s2, o0, o1), pt(ik), pt(ok))
+
+    def TT(o, ok, a, b, ik, op):
+        return emit("V", lambda: v.tensor_tensor(o, a, b, op), pt(ik), pt(ok))
+
+    def CP(o, ok, i, ik):
+        return emit("V", lambda: v.tensor_copy(o, i), pt(ik), pt(ok))
+
+    def ACT(o, ok, i, ik, f=AF.Copy, **kw):
+        return emit("S", lambda: s.activation(o, i, f, **kw), pt(ik), pt(ok))
+
+    def TR(o, ok, i, ik):
+        return emit("V", lambda: v.transpose(o, i), pt(ik), pt(ok))
+
+    def RED(o, ok, i, ik, op):
+        return emit("V", lambda: v.tensor_reduce(o, i, AxisListType.X, op), pt(ik), pt(ok))
+
+    def FILL(ap, ok, c):
+        return emit("V", lambda: v.memset(ap, c), [], pt(ok))
+
+    def QT(q, a, b, i, ik):
+        return emit("V", lambda: v.quantize_mx(*K(q, a, b), i), pt(ik), [q, "s" + q])
+
+    def MM(bank, n, w, wa, m, ma):
+        (wt, ws), (mt, ms) = K(w, wa, wa + 128), K(m, ma, ma + n)
+        o = T["ps%d" % bank][:, 0:n]
+        return emit("T", lambda: g.tensor.matmul_mx(o, wt, ws, mt, ms, True, True), [w, "s" + w, m, "s" + m], ["ps%d" % bank])
+
+    def PICK(o, i, lst, lk):
+        (oc, osc), (ic, isc) = K(o, 0, 256), K(i, 0, 256)
+        emit("V", lambda: v.tensor_copy(oc.bitcast(dt.uint32), ic.bitcast(dt.uint32).indirect(lst)), [i, lk], [o])
+        emit("S", lambda: s.activation(osc, isc.indirect(lst), AF.Copy), ["s" + i, lk], ["s" + o])
+
+    def IOTA(ap, ok, pat, base, cm, f=True):
+        if f:
+            return emit("G", lambda: g.iota(ap, pat, base, cm, allow_small_or_imprecise_dtypes=True), [], pt(ok))
+        return emit("G", lambda: g.iota(ap, pat, base, cm), [], pt(ok))
+
+    def AFF(o, ok, i, ik, pat, op, base, cm):
+        return emit("G", lambda: g.affine_select(o, i, pat, op, 0.0, base, cm), pt(ik), pt(ok))
+
+    emit("Y", lambda: g.sync.dma_start(T.xs[:], T.x[:]), [], ["xs"], dma=True)
+    emit("S", lambda: s.dma_start(T.us[:], T.u[:]), [], ["us"], dma=True)
+    emit("Y", lambda: g.sync.dma_start(T.qw[:, 0:512].bitcast(dt.uint8), T.wc[:, 0:2048]), [], ["qw"], dma=True)
+    emit("Y", lambda: g.sync.dma_start(T.sqw[:, 0:512], T.ws[:, 0:512]), [], ["sqw"], dma=True)
+    emit("Y", lambda: g.sync.dma_start(T.vs[:], T.v[:]), [], ["vs"], dma=True)
+
+    FILL(T.one[:], "one", 1.0)
+    IOTA(T.pI[:], "pI", [[0, 1]], 0, 1, False)
+    IOTA(T.io8[:], "io8", [[1, 8]], 0, 0)
+    IOTA(I("ni"), "ni", [[16, 16]], 0, 1, False)
+    AFF(T.dyb[:], "dyb", T.one[:], "one", [[0, 8], [-8, 16]], A.is_ge, 0, 1)
+    AFF(T.dy0[:], "dy0", T.dyb[:], "dyb", [[0, 8], [8, 16]], A.is_ge, 3, -1)
+    AFF(T.dyc[:], "dyc", T.one[:], "one", [[0, 8], [-8, 16]], A.is_ge, -4, 1)
+    AFF(T.dy1[:], "dy1", T.dyc[:], "dyc", [[0, 8], [8, 16]], A.is_ge, 7, -1)
+    AFF(T.dya[:], "dya", T.one[:], "one", [[0, 4], [-4, 2], [-8, 16]], A.is_ge, 0, 1)
+    AFF(T.dy[:], "dy", T.dya[:], "dya", [[0, 4], [4, 2], [8, 16]], A.is_ge, 3, -1)
+    IOTA(T.bp[:], "bp0", [[1, 128]], -1, 0)
+    AFF(T.idn[:], "idn", T.one[:], "one", [[-1, 128]], A.is_equal, 0, 1)
+    AFF(T.prm[:], "prm0", T.one[:], "one", [[-16, 4], [0, 2], [-1, 16]], A.is_equal, 0, 1)
+    AFF(T.prm[:, 0:16], "prm", T.one[:, 0:16], ["one", "prm0"], [[-1, 16]], A.is_equal, -112, 1)
+    IOTA(T.br[:], "br", [[1, 256]], -1, 0)
+    IOTA(T.ti[:], "ti", [[16, 2], [32, 8], [1, 16]], 0, 0, False)
+
+    FILL(T.zer[:], "zer", 0.0)
+    ACT(T.cl[:, 1536:2048], "cl0S", T.zer[:, 0:512], "zer")
+    ACT(T.cl[:, 2048:2560], "cl0S", T.zer[:, 0:512], "zer")
+    ACT(T.mt[:], "mt0", T.zer[:, 0:512], "zer")
+    ACT(T.pwf[:], "pwf", T.io8[:], "io8", AF.Exp, scale=math.log(2.0))
+    FILL(T.cl[:, 0:1536], "cl0", 0.0)
+    TS(T.pi16[:], "pi16", T.pI[:], "pI", 15, None, A.bitwise_and)
+    TS(T.pi8[:], "pi8", T.pI[:], "pI", 7, None, A.bitwise_and)
+    TS(T.pi4[:], "pi4", T.pI[:], "pI", 3, None, A.bitwise_and)
+    TS(T.pih[:], "pih", T.pI[:], "pI", 4, 1, A.arith_shift_right, A.bitwise_and)
+    TS(T.cf[:, 5:6], "cf5", T.pI[:], "pI", 1.0, None, A.mult)
+    TS(T.cf[:, 4:5], "cf4", T.pi16[:], "pi16", 1.0, None, A.mult)
+    TT(T.cf[:, 3:4], "cf3", T.cf[:, 4:5], T.cf[:, 5:6], ["cf4", "cf5"], A.subtract)
+    TS(I("nj"), "nj", I("ni"), ["ni", "cf3"], T.cf[:, 3:4], None, A.add)
+    TS(I("nk"), "nk", I("nj"), "nj", 7, None, A.bitwise_and)
+    TS(I("ok1"), "ok1", I("nj"), "nj", 3, None, A.arith_shift_right)
+    TS(I("oi"), "oi", I("nk"), "nk", 32.0, None, A.mult)
+    TT(I("nk"), "nk", I("oi"), I("ok1"), ["oi", "ok1"], A.add)
+    CP(T.nl[:], "nl", I("nk"), "nk")
+    for h in range(4):
+        TS(T.mk[:, h:h + 1], "mk", T.pi4[:], "pi4", float(h), None, A.is_equal)
+    TS(T.c8[:, 0:1], "c80", T.pI[:], "pI", 16.0, 8.0, A.is_lt, A.mult)
+    TS(T.c8[:, 1:2], "c81", T.pI[:], "pI", 16.0, -10.0, A.is_lt, A.mult)
+    emit("V", lambda: v.memset(T.wtr[:], 0), [], ["wtr"])
+    CP(T.pow[:], "pow", T.pwf[:], "pwf")
+    for y, nm in ((0, "dy0"), (1, "dy1")):
+        for G in range(8):
+            o = 1536 + 512 * y + 64 * G + G % 4
+            ACT(T.cl[:, o:o + 61:4], "clS", T[nm][:, 16 * G:16 * G + 16], [nm, "cl0S"])
+
+    QT("qx", 0, 256, T.xs[:], "xs")
+    QT("qu", 0, 128, T.us[:], "us")
+    PICK("qn0", "qx", T.nl[:, 0:16], "nl")
+    ACT(T.cg[:], "cg0", T.zer[:], "zer")
+    ACT(T.ce[:], "ce0", T.zer[:], "zer")
+    ACT(T.win[:], "win", T.zer[:, 0:512], "zer")
+    CP(T.cl[:, 0:512:4], "clV", T.dy[:], ["dy", "cl0"])
+    CP(T.cl[:, 513:1024:4], "clV", T.dy[:], "dy")
+    for k in range(4):
+        o = 1024 + 128 * k + 2 + k % 2
+        CP(T.cl[:, o:o + 125:4], "clV", T.dy[:, 32 * k:32 * k + 32], "dy")
+    QT("qcl", 0, 384, T.cl[:, 0:1536], "clV")
+    QT("qcr", 0, 256, T.cl[:, 1536:2560], "clS")
+    TS(T.dT[:, 0:8], "dT", T.io8[:], "io8", 256.0, 257.0, A.mult, A.add)
+    TS(T.dT[:, 8:16], "dT", T.io8[:], "io8", 256.0, 257.0, A.mult, A.add)
+    TS(T.cf[:, 2:3], "cf2", T.pi8[:], "pi8", 1.0, None, A.mult)
+    TS(T.pen[:], "pen", T.io8[:], ["io8", "cf2"], T.cf[:, 2:3], float(BIG), A.not_equal, A.mult)
+    TS(T.cf[:, 1:2], "cf1", T.pih[:], "pih", 128.0, None, A.mult)
+    TS(T.bp[:], "bp", T.bp[:], ["bp0", "cf1"], T.cf[:, 1:2], None, A.add)
+
+    def key_constants():
+        TS(T.cm[:, 0:1], "cm", T.pih[:], "pih", 0.0, -1.0, A.is_equal, A.mult)
+        TS(T.cm[:, 1:2], "cm", T.pih[:], "pih", -1.0, None, A.mult)
+        TS(W("own"), "own", I("nj"), "nj", 16.0, None, A.add)
+
+    def order_constants():
+        TS(T.cf[:, 0:1], "cf0", T.pih[:], "pih", 16.0, 255.0, A.mult, A.add)
+        TS(T.cf[:, 6:7], "cf6", T.pih[:], "pih", 16.0, None, A.mult)
+        TS(T.tj[:], "tj", T.ti[:], ["ti", "cf6"], T.cf[:, 6:7], None, A.add)
+        TS(T.ti[:], "ti", T.tj[:], "tj", 255, None, A.bitwise_and)
+        CP(T.vrow[:], "vrow", T.ti[:], "ti")
+
+    def column_constants():
+        CP(T.vcol[:], "vcol", T.ti[:], "ti")
+        TS(I("oi"), "oi", I("nj"), "nj", 31, None, A.bitwise_and)
+        TS(I("oj"), "oj", I("nj"), "nj", 5, None, A.arith_shift_right)
+        TS(I("ok1"), "ok1", I("oi"), "oi", 8.0, None, A.mult)
+        TT(I("oi"), "oi", I("ok1"), I("oj"), ["ok1", "oj"], A.add)
+        CP(T.ol[:], "ol", I("oi"), "oi")
+        QT("qv", 0, 128, T.vs[:], "vs")
+
+    rid, pid, _ = topo.addr(nxt)
+    eng = topo.engines(core, nxt)
+    half = len(eng) // 2
+    mask_c, mask_s = sum(1 << e for e in eng[:half]), sum(1 << e for e in eng[half:])
+    n_in = len(topo.engines(prv, core))
+
+    def level(w, d, lst):
+        for h in range(4):
+            a = slice(32 * h, 32 * h + 32)
+            emit("V", lambda: v.tensor_tensor_scan(T.tp[:, a], T[w][:, a], T[d][:, a], -1.0, A.max, A.add), [w, d], ["tp"])
+        TT(T.mm[:], "mm", T.pen[:].indirect(T[lst][:, 0:8]), T.tp[:], ["pen", lst, "tp"], A.max)
+        RED(T.mv[:], "mv", T.mm[:], "mm", A.min)
+        TS(T.rep[:], "rep", T.zer[:, 0:32], ["zer", "mv"], T.mv[:, 0:1], None, A.add)
+        TR(T.trp[:], "trp", T.rep[:], "rep")
+
+    def waits(tab, lst):
+        TT(T[tab][:], tab, T.trp[:, 0:16], T.trp[:, 16:32], "trp", A.min)
+        TS(T.wt[:], "wt", T[tab][:, 0:8], tab, TMASK, None, A.bitwise_and)
+        TT(T.wp[:], "wp", T.wt[:].indirect(T[lst][:, 0:8]), T.bp[:], ["wt", lst, "bp"], A.add)
+
+    for r in range(NR):
+        last = r == NR - 1
+        q = "qn%d" % r
+        if r:
+            QT(q, 0, 256, T.X[:], ["X0", "X1", "XS0"])
+        for hf in range(2):
+            MM(hf, 128, q, 128 * hf, "qu", 0)
+            for i in range(3):
+                TS(T.sb[:, 16 * i + 8 * hf:16 * i + 8 * hf + 8], "sb", T["ps%d" % hf][:, i:128:16], "ps%d" % hf, 0.0, float(4 >> i), A.is_gt, A.mult)
+        TT(W("s1"), "s1", T.sb[:, 0:16], T.sb[:, 16:32], "sb", A.add)
+        TT(W("sn"), "sn", W("s1"), T.sb[:, 32:48], ["s1", "sb"], A.add)
+        for h in range(4):
+            if h < 2:
+                TS(T.mt[:, 16 * h:16 * h + 16], "mt", W("sn"), ["sn", "mk", "mt0"], T.mk[:, h:h + 1], None, A.mult)
+            else:
+                ACT(T.mt[:, 16 * h:16 * h + 16], "mtS", W("sn"), ["sn", "mk", "mt0"], scale=T.mk[:, h:h + 1])
+        QT("qm", 0, 128, T.mt[:], ["mt", "mtS"])
+        for k in range(3):
+            MM(2 + k, 128, "qcl", 128 * k, "qm", 0)
+        for k in range(2):
+            MM(5 + k, 128, "qcr", 128 * k, "qm", 0)
+        if r == 0:
+            fq = "qx"
+            ACT(T.cg[:, 3:512:4], "cg", T.prm[:], ["prm", "cg0"])
+            ACT(T.ce[:, 3:512:4], "ce", T.idn[:], ["idn", "ce0"])
+        else:
+            fq = "qp%d" % r
+            PICK(fq, q, T.ol[:, 0:16], "ol")
+        CP(T.l0[:], "l0", T.ps2[:, 0:16:2], "ps2")
+        CP(T.da[:], "da", T.dT[:, 0:8].indirect(T.l0[:, 0:8]), ["dT", "l0"])
+        CP(T.l1[:], "l1", T.ps3[:, 0:16:2], "ps3")
+        ACT(T.db[:], "db", T.dT[:, 0:8].indirect(T.l1[:, 0:8]), ["dT", "l1"])
+        for y in range(2):
+            for hf in range(2):
+                ACT(W("srf", 64 * hf, 64 * hf + 64, 8 * y, 8 * y + 8), "srf", T["ps%d" % (5 + y)][64 * hf:64 * hf + 64, hf:16:2], ["ps%d" % (5 + y), "c80"],
+                    AF.Identity, bias=T.c8[64 * hf:64 * hf + 64, 0:1])
+        level("bp", "da", "l0")
+        waits("tab0", "l1")
+        CP(T.l2[:], "l2", T.ps4[:, 0:16:2], "ps4")
+        ACT(T.dc[:], "dc", T.dT[:, 0:8].indirect(T.l2[:, 0:8]), ["dT", "l2"])
+        CP(T.lr[:], "lr", W("srf"), "srf")
+        ACT(T.dr[:], "dr", T.dT[:].indirect(T.lr[:, 0:16]), ["dT", "lr"])
+        ACT(W("inv"), "inv", W("srf"), ["srf", "c81"], AF.Exp, bias=T.c8[:, 1:2], scale=-math.log(2.0))
+        level("wp", "db", "l1")
+        waits("tab1", "l2")
+        if r == 0:
+            for b in range(4):
+                QT("qcg", 128 * b, 128 * b + 128, T.cg[:, 3 - b:515 - b], "cg")
+            for b in range(4):
+                QT("qce", 128 * b, 128 * b + 128, T.ce[:, 3 - b:515 - b], "ce")
+        for j in range(8):
+            b, src, bk = j % 4, ("qcg", "qce")[j // 4], (7, 0, 1, 2, 3, 4, 5, 6)[j]
+            MM(bk, 256, src, 128 * b, fq, 0)
+            if j < 4:
+                ACT(T.G[:, 272 * b + 16:272 * b + 272], "G%d" % b, T["ps%d" % bk][:, 0:256], "ps%d" % bk, scale=0.5)
+            else:
+                ACT(T.F[:, 256 * b:256 * b + 256], "F%d" % b, T["ps%d" % bk][:, 0:256], "ps%d" % bk, scale=0.5)
+        level("wp", "dc", "l2")
+        TT(T.tabr[64:128, :], "tabr2", T.trp[64:128, 0:16], T.trp[64:128, 16:32], "trp", A.min)
+        CP(T.tabr[0:32, :], "tabr0", T.tab0[0:32, :], "tab0")
+        CP(T.tabr[32:64, :], "tabr1", T.tab1[32:64, :], "tab1")
+        tb = ["tabr0", "tabr1", "tabr2"]
+        TS(T.wtr[:, 0:8], "wtr", T.tabr[:, 0:8], tb, TMASK, None, A.bitwise_and)
+        TT(T.wr[:], "wr", T.wtr[:].indirect(T.lr[:, 0:16]), T.br[:], ["wtr", "lr", "br"], A.add)
+        for h in range(8):
+            a = slice(32 * h, 32 * h + 32)
+            emit("V", lambda: v.tensor_tensor_scan(T.key[:, a], T.wr[:, a], T.dr[:, a], -1.0, A.max, A.add), ["wr", "dr"], ["key"])
+        CP(T.key[:, 256:272], "keyx", T.key[:, 0:16], "key")
+        TR(T.kt[:, 0:256], "kt", T.key[:, 0:256], "key")
+        TR(T.kt[:, 256:512], "kt", T.key[:, 16:272], ["key", "keyx"])
+        if r == 0:
+            key_constants()
+        TS(W("ka"), "ka", T.kt[:, 0:512:32], ["kt", "cm"], T.cm[:, 0:1], None, A.mult)
+        TS(W("kb"), "kb", T.kt[:, 16:512:32], ["kt", "cm"], T.cm[:, 1:2], None, A.mult)
+        TT(W("kn"), "kn", W("ka"), W("kb"), ["ka", "kb"], A.add)
+        for w in range(VUNITS, 16):
+            j = 256 * (w - VUNITS)
+            ACT(T.js[:, j:j + 256], "accS", T.key[:, 0:256], ["key", "kn"], AF.Sign, bias=W("kn", 0, 128, w, w + 1), accum_out=T.acc[:, w:w + 1])
+        TS(I("fi"), "fi", T.tabr[:], tb, 255, None, A.bitwise_and)
+        TS(T.prs[:], "prs", T.tabr[:, 0:8], tb, float(BIG), None, A.is_lt)
+        CP(T.tin[:, 0:16], "tin", I("fi"), "fi")
+        CP(T.tin[:, 16:32], "tin", I("fi"), "fi")
+        TT(T.prw[:], "prw", T.prs[:], T.pow[:], ["prs", "pow"], A.mult)
+        TR(T.tout[:], "tout", T.tin[:], "tin")
+        RED(T.bb[:], "bb", T.prw[:], "prw", A.add)
+        CP(T.fl[:], "fl", T.tout[:, 0:2], "tout")
+        TS(I("pf"), "pf", W("inv"), ["inv", "bb"], T.bb[:, 0:1], -0.495, A.mult, A.add)
+        TT(W("dif"), "dif", W("srf"), W("own"), ["srf", "own"], A.subtract)
+        TS(I("pg"), "pg", I("pf"), "pf", 1, None, A.bitwise_and)
+        TT(W("ph"), "ph", I("pg"), W("dif"), ["pg", "dif"], A.mult)
+        TT(W("pq"), "pq", W("ph"), W("own"), ["ph", "own"], A.add)
+        CP(T.gl[:], "gl", W("pq"), "pq")
+        for t in range(4):
+            ACT(T.G[:, 272 * t:272 * t + 16], "Gf%d" % t, T.G[:, 272 * t + 16:272 * t + 272].indirect(T.fl[:, 0:1]), ["G%d" % t, "fl"])
+        for t in range(4):
+            ACT(T.Gp[:, 256 * t:256 * t + 256], "Gp%d" % t, T.G[:, 272 * t:272 * t + 272].indirect(T.gl[:, 0:16]), ["G%d" % t, "Gf%d" % t, "gl"])
+        if r == 0:
+            order_constants()
+        for w in range(VUNITS + 1):
+            if w < VUNITS:
+                j = "jv%d" % w
+                TS(T[j][:], j, T.key[:, 0:256], ["key", "kn"], W("kn", 0, 128, w, w + 1), 0.0, A.add, A.is_lt)
+            if w:
+                j = "jv%d" % (w - 1)
+                RED(T.acr[:, w - 1:w], "acr", T[j][:], j, A.add)
+        TS(T.acc[:, 0:VUNITS], "accV", T.acr[:, 0:VUNITS], "acr", -2.0, 255.0, A.mult, A.add)
+        ak = ["accV", "accS"]
+        TS(I("ri"), "ri", T.acc[:], ak, -0.5, 127.5, A.mult, A.add)
+        TS(W("ry"), "ry", T.acc[:], ak + ["cf0"], -1.0, T.cf[:, 0:1], A.mult, A.add)
+        TS(I("rx"), "rx", I("ri"), "ri", 15, None, A.bitwise_and)
+        TT(W("rz"), "rz", W("ry"), I("rx"), ["ry", "rx"], A.subtract)
+        CP(T.pl[:], "pl", W("rz"), "rz")
+        emit("V", lambda: v.tensor_copy(T.win[:].indirect(T.pl[:, 0:16]), T.vrow[:]), ["pl", "vrow", "win"], ["win"])
+        TR(T.wtt[:], "wtt", T.win[:], "win")
+        TT(W("of"), "of", T.wtt[:, 0:512:32], T.wtt[:, 16:512:32], "wtt", A.add)
+        CP(T.ou[:], "ou", W("of"), "of")
+        for t in range(4):
+            ACT(T.gz[:, 128 * t:128 * t + 128], "gz%d" % t, T.Gp[:, 256 * t:256 * t + 256].indirect(T.ou[:, 0:8]), ["Gp%d" % t, "ou"])
+        for t in range(4):
+            TT(T.Z[:, t:512:4], "Z", T.F[:, 256 * t:256 * t + 256].indirect(T.ou[:, 0:8]), T.gz[:, 128 * t:128 * t + 128], ["F%d" % t, "ou", "gz%d" % t], A.add)
+        z, a = "qz%d" % r, "qa%d" % r
+        QT(z, 0, 128, T.Z[:], "Z")
+        need("G", toks_of("G", [z], []))
+        (zc, zs), (ac, asc) = K(z, 0, 128), K(a, 0, 128)
+        g.remote_dma(ac.bitcast(dt.uint8), zc.bitcast(dt.uint8), T.sem["arr%d" % r], T.sem.sent, pid, rid, mask_c)
+        g.remote_dma(asc, zs, T.sem["arr%d" % r], T.sem.sent, pid, rid, mask_s)
+        landed("arr%d" % r, n_in, [a, "s" + a])
+        for t in range(4):
+            if t < 2:
+                TS(T.X[:, t:512:4], "X0", T.F[:, 256 * t:256 * t + 256].indirect(T.ou[:, 8:16]), ["F%d" % t, "ou"], 2.0, None, A.mult)
+            else:
+                ACT(T.X[:, t:512:4], "XS0", T.F[:, 256 * t:256 * t + 256].indirect(T.ou[:, 8:16]), ["F%d" % t, "ou"], scale=2.0)
+        if r == 0:
+            column_constants()
+        if last:
+            CP(T.rl[:], "rl", I("ri"), "ri")
+            emit("V", lambda: v.tensor_copy(T.opw[:].indirect(T.rl[:, 0:16]), T.vcol[:]), ["rl", "vcol"], ["opw"])
+            emit("Y", lambda: g.sync.dma_start(T.op[:], T.opw[0:128:16, :]), ["opw"], ["op"], dma=True)
+        for b in range(4):
+            MM(b, 128, "qw", 128 * b, a, 0)
+            MM(4 + b, 128, "qce", 128 * b, a, 0)
+            ACT(T.hr[:, 128 * b:128 * b + 128], "hr%d" % b, T["ps%d" % b][:, 0:128], "ps%d" % b, scale=0.0078125)
+            TT(T.X[:, 512 + b:1024:4], "X1", T.hr[:, 128 * b:128 * b + 128], T["ps%d" % (4 + b)][:, 0:128], ["hr%d" % b, "ps%d" % (4 + b)], A.add)
+    QT("qn3", 0, 256, T.X[:], ["X0", "X1", "XS0"])
+    PICK("qp3", "qn3", T.ol[:, 0:16], "ol")
+    MM(0, 256, "qv", 0, "qp3", 0)
+    yc, _ = K("qp3", 0, 256)
+    emit("Y", lambda: g.sync.dma_start(T.oc[:, 0:1024], yc.bitcast(dt.uint8)), ["qp3"], ["oc"], dma=True)
+    for k in range(4):
+        emit("Y" if k < 2 else "S", lambda: (g.sync if k < 2 else s).dma_start(T.osc[4 * k:4 * k + 4, 0:256], T.sqp[32 * k:32 * k + 4, 256 * NR:256 * NR + 256]),
+             ["sqp3"], ["osc%d" % k], dma=True)
+    CP(T.ysb[:], "ysb", T.ps0[:, 0:256], "ps0")
+    emit("Y", lambda: g.sync.dma_start(T.y[:], T.ysb[:]), ["ysb"], ["y"], dma=True)
+    for k in range(nd[0]):
+        g.wait_ge(T.sem["ld%d" % k], 16)
+    g.wait_ge(T.sem.sent, NR * len(eng))
+    for k in "VSTG":
+        g.wait_ge(T.sem["c" + k], count[k])

@@ -138,6 +138,8 @@ def rank_program(g, core, T, topo):
     place = {"qcl": ("qc", 0), "qcr": ("qc", 384), "qce": ("qc", 640), "qcg": ("qc", 1152)}
     for k in range(NR + 1):
         place["qn%d" % k] = ("qn", 256 * k)
+        place["na%d" % k] = ("qn", 256 * k)
+        place["nb%d" % k] = ("qn", 256 * k + 128)
         place["qp%d" % k] = ("qp", 256 * k)
         place["qz%d" % k] = ("qz", 128 * k)
         place["qa%d" % k] = ("qa", 128 * k)
@@ -180,10 +182,10 @@ def rank_program(g, core, T, topo):
         o = T["ps%d" % bank][:, 0:n]
         return emit("T", lambda: g.tensor.matmul_mx(o, wt, ws, mt, ms, True, True), [w, "s" + w, m, "s" + m], ["ps%d" % bank])
 
-    def PICK(o, i, lst, lk):
+    def PICK(o, i, lst, lk, ok, ik):
         (oc, osc), (ic, isc) = K(o, 0, 256), K(i, 0, 256)
-        emit("V", lambda: v.tensor_copy(oc.bitcast(dt.uint32), ic.bitcast(dt.uint32).indirect(lst)), [i, lk], [o])
-        emit("S", lambda: s.activation(osc, isc.indirect(lst), AF.Copy), ["s" + i, lk], ["s" + o])
+        emit("V", lambda: v.tensor_copy(oc.bitcast(dt.uint32), ic.bitcast(dt.uint32).indirect(lst)), ik + [lk], ok)
+        emit("S", lambda: s.activation(osc, isc.indirect(lst), AF.Copy), ["s" + k for k in ik] + [lk], ["s" + k for k in ok])
 
     def IOTA(ap, ok, pat, base, cm, f=True):
         if f:
@@ -239,8 +241,6 @@ def rank_program(g, core, T, topo):
         TS(T.mk[:, h:h + 1], "mk", T.pi4[:], "pi4", float(h), None, A.is_equal)
     TS(T.c8[:, 0:1], "c80", T.pI[:], "pI", 16.0, 8.0, A.is_lt, A.mult)
     TS(T.c8[:, 1:2], "c81", T.pI[:], "pI", 16.0, -10.0, A.is_lt, A.mult)
-    emit("V", lambda: v.memset(T.wtr[:], 0), [], ["wtr"])
-    CP(T.pow[:], "pow", T.pwf[:], "pwf")
     for y, nm in ((0, "dy0"), (1, "dy1")):
         for G in range(8):
             o = 1536 + 512 * y + 64 * G + G % 4
@@ -248,7 +248,7 @@ def rank_program(g, core, T, topo):
 
     QT("qx", 0, 256, T.xs[:], "xs")
     QT("qu", 0, 128, T.us[:], "us")
-    PICK("qn0", "qx", T.nl[:, 0:16], "nl")
+    PICK("qn0", "qx", T.nl[:, 0:16], "nl", ["na0", "nb0"], ["qx"])
     ACT(T.cg[:], "cg0", T.zer[:], "zer")
     ACT(T.ce[:], "ce0", T.zer[:], "zer")
     ACT(T.win[:], "win", T.zer[:, 0:512], "zer")
@@ -259,12 +259,16 @@ def rank_program(g, core, T, topo):
         CP(T.cl[:, o:o + 125:4], "clV", T.dy[:, 32 * k:32 * k + 32], "dy")
     QT("qcl", 0, 384, T.cl[:, 0:1536], "clV")
     QT("qcr", 0, 256, T.cl[:, 1536:2560], "clS")
-    TS(T.dT[:, 0:8], "dT", T.io8[:], "io8", 256.0, 257.0, A.mult, A.add)
-    TS(T.dT[:, 8:16], "dT", T.io8[:], "io8", 256.0, 257.0, A.mult, A.add)
-    TS(T.cf[:, 2:3], "cf2", T.pi8[:], "pi8", 1.0, None, A.mult)
-    TS(T.pen[:], "pen", T.io8[:], ["io8", "cf2"], T.cf[:, 2:3], float(BIG), A.not_equal, A.mult)
-    TS(T.cf[:, 1:2], "cf1", T.pih[:], "pih", 128.0, None, A.mult)
-    TS(T.bp[:], "bp", T.bp[:], ["bp0", "cf1"], T.cf[:, 1:2], None, A.add)
+
+    def path_constants():
+        TS(T.dT[:, 0:8], "dT", T.io8[:], "io8", 256.0, 257.0, A.mult, A.add)
+        TS(T.dT[:, 8:16], "dT", T.io8[:], "io8", 256.0, 257.0, A.mult, A.add)
+        TS(T.cf[:, 2:3], "cf2", T.pi8[:], "pi8", 1.0, None, A.mult)
+        TS(T.pen[:], "pen", T.io8[:], ["io8", "cf2"], T.cf[:, 2:3], float(BIG), A.not_equal, A.mult)
+        TS(T.cf[:, 1:2], "cf1", T.pih[:], "pih", 128.0, None, A.mult)
+        TS(T.bp[:], "bp", T.bp[:], ["bp0", "cf1"], T.cf[:, 1:2], None, A.add)
+        emit("V", lambda: v.memset(T.wtr[:], 0), [], ["wtr"])
+        CP(T.pow[:], "pow", T.pwf[:], "pwf")
 
     def key_constants():
         TS(T.cm[:, 0:1], "cm", T.pih[:], "pih", 0.0, -1.0, A.is_equal, A.mult)
@@ -288,10 +292,32 @@ def rank_program(g, core, T, topo):
         QT("qv", 0, 128, T.vs[:], "vs")
 
     rid, pid, _ = topo.addr(nxt)
-    eng = topo.engines(core, nxt)
-    half = len(eng) // 2
-    mask_c, mask_s = sum(1 << e for e in eng[:half]), sum(1 << e for e in eng[half:])
-    n_in = len(topo.engines(prv, core))
+    mask = topo.mask(core, nxt)
+    n_out, n_in = 2 * len(topo.engines(core, nxt)), 2 * len(topo.engines(prv, core))
+
+    def symbols(k, hf):
+        q = ("na%d", "nb%d")[hf] % k
+        if k:
+            QT(q, 0, 128, T.X[:, 512 * hf:512 * hf + 512], [["X0", "XS0"], ["X1"]][hf])
+        if k == NR:
+            MM(hf, 128, "qv", 0, q, 0)
+            return
+        MM(hf, 128, q, 0, "qu", 0)
+        a, b = 8 * hf, 8 * hf + 8
+        for i in range(3):
+            TS(T.sb[:, 16 * i + a:16 * i + b], "sb%d" % hf, T["ps%d" % hf][:, i:128:16], "ps%d" % hf, 0.0, float(4 >> i), A.is_gt, A.mult)
+        TT(W("s1", 0, 128, a, b), "s1%d" % hf, T.sb[:, a:b], T.sb[:, 16 + a:16 + b], "sb%d" % hf, A.add)
+        TT(W("sn", 0, 128, a, b), "sn%d" % hf, W("s1", 0, 128, a, b), T.sb[:, 32 + a:32 + b], ["s1%d" % hf, "sb%d" % hf], A.add)
+        for h in range(4):
+            o, sn = T.mt[:, 16 * h + a:16 * h + b], W("sn", 0, 128, a, b)
+            if h < 2:
+                TS(o, "mt%dv" % hf, sn, ["sn%d" % hf, "mk", "mt0"], T.mk[:, h:h + 1], None, A.mult)
+            else:
+                ACT(o, "mt%ds" % hf, sn, ["sn%d" % hf, "mk", "mt0"], scale=T.mk[:, h:h + 1])
+
+    def y_columns(hf):
+        for h in range(8):
+            CP(T.ysb[:, 32 * h + 16 * hf:32 * h + 16 * hf + 16], "ysb", T["ps%d" % hf][:, h:128:8], "ps%d" % hf)
 
     def level(w, d, lst):
         for h in range(4):
@@ -302,39 +328,31 @@ def rank_program(g, core, T, topo):
         TS(T.rep[:], "rep", T.zer[:, 0:32], ["zer", "mv"], T.mv[:, 0:1], None, A.add)
         TR(T.trp[:], "trp", T.rep[:], "rep")
 
-    def waits(tab, lst):
+    def waits(k, lst):
+        tab = "tab%d" % k
         TT(T[tab][:], tab, T.trp[:, 0:16], T.trp[:, 16:32], "trp", A.min)
         TS(T.wt[:], "wt", T[tab][:, 0:8], tab, TMASK, None, A.bitwise_and)
+        CP(T.tabr[32 * k:32 * k + 32, :], "tabr%d" % k, T[tab][32 * k:32 * k + 32, :], tab)
         TT(T.wp[:], "wp", T.wt[:].indirect(T[lst][:, 0:8]), T.bp[:], ["wt", lst, "bp"], A.add)
 
     for r in range(NR):
         last = r == NR - 1
-        q = "qn%d" % r
-        if r:
-            QT(q, 0, 256, T.X[:], ["X0", "X1", "XS0"])
-        for hf in range(2):
-            MM(hf, 128, q, 128 * hf, "qu", 0)
-            for i in range(3):
-                TS(T.sb[:, 16 * i + 8 * hf:16 * i + 8 * hf + 8], "sb", T["ps%d" % hf][:, i:128:16], "ps%d" % hf, 0.0, float(4 >> i), A.is_gt, A.mult)
-        TT(W("s1"), "s1", T.sb[:, 0:16], T.sb[:, 16:32], "sb", A.add)
-        TT(W("sn"), "sn", W("s1"), T.sb[:, 32:48], ["s1", "sb"], A.add)
-        for h in range(4):
-            if h < 2:
-                TS(T.mt[:, 16 * h:16 * h + 16], "mt", W("sn"), ["sn", "mk", "mt0"], T.mk[:, h:h + 1], None, A.mult)
-            else:
-                ACT(T.mt[:, 16 * h:16 * h + 16], "mtS", W("sn"), ["sn", "mk", "mt0"], scale=T.mk[:, h:h + 1])
-        QT("qm", 0, 128, T.mt[:], ["mt", "mtS"])
+        if r == 0:
+            symbols(0, 0)
+        symbols(r, 1)
+        QT("qm", 0, 128, T.mt[:], ["mt0v", "mt0s", "mt1v", "mt1s"])
         for k in range(3):
             MM(2 + k, 128, "qcl", 128 * k, "qm", 0)
         for k in range(2):
             MM(5 + k, 128, "qcr", 128 * k, "qm", 0)
         if r == 0:
+            path_constants()
             fq = "qx"
             ACT(T.cg[:, 3:512:4], "cg", T.prm[:], ["prm", "cg0"])
             ACT(T.ce[:, 3:512:4], "ce", T.idn[:], ["idn", "ce0"])
         else:
             fq = "qp%d" % r
-            PICK(fq, q, T.ol[:, 0:16], "ol")
+            PICK(fq, "qn%d" % r, T.ol[:, 0:16], "ol", [fq], ["na%d" % r, "nb%d" % r])
         CP(T.l0[:], "l0", T.ps2[:, 0:16:2], "ps2")
         CP(T.da[:], "da", T.dT[:, 0:8].indirect(T.l0[:, 0:8]), ["dT", "l0"])
         CP(T.l1[:], "l1", T.ps3[:, 0:16:2], "ps3")
@@ -344,14 +362,15 @@ def rank_program(g, core, T, topo):
                 ACT(W("srf", 64 * hf, 64 * hf + 64, 8 * y, 8 * y + 8), "srf", T["ps%d" % (5 + y)][64 * hf:64 * hf + 64, hf:16:2], ["ps%d" % (5 + y), "c80"],
                     AF.Identity, bias=T.c8[64 * hf:64 * hf + 64, 0:1])
         level("bp", "da", "l0")
-        waits("tab0", "l1")
+        waits(0, "l1")
         CP(T.l2[:], "l2", T.ps4[:, 0:16:2], "ps4")
         ACT(T.dc[:], "dc", T.dT[:, 0:8].indirect(T.l2[:, 0:8]), ["dT", "l2"])
         CP(T.lr[:], "lr", W("srf"), "srf")
         ACT(T.dr[:], "dr", T.dT[:].indirect(T.lr[:, 0:16]), ["dT", "lr"])
+        ACT(T.dr[:, 31:256:32], "dr", T.dr[:, 31:256:32], "dr", AF.Identity, bias=-float(BIG))
         ACT(W("inv"), "inv", W("srf"), ["srf", "c81"], AF.Exp, bias=T.c8[:, 1:2], scale=-math.log(2.0))
         level("wp", "db", "l1")
-        waits("tab1", "l2")
+        waits(1, "l2")
         if r == 0:
             for b in range(4):
                 QT("qcg", 128 * b, 128 * b + 128, T.cg[:, 3 - b:515 - b], "cg")
@@ -366,14 +385,11 @@ def rank_program(g, core, T, topo):
                 ACT(T.F[:, 256 * b:256 * b + 256], "F%d" % b, T["ps%d" % bk][:, 0:256], "ps%d" % bk, scale=0.5)
         level("wp", "dc", "l2")
         TT(T.tabr[64:128, :], "tabr2", T.trp[64:128, 0:16], T.trp[64:128, 16:32], "trp", A.min)
-        CP(T.tabr[0:32, :], "tabr0", T.tab0[0:32, :], "tab0")
-        CP(T.tabr[32:64, :], "tabr1", T.tab1[32:64, :], "tab1")
         tb = ["tabr0", "tabr1", "tabr2"]
         TS(T.wtr[:, 0:8], "wtr", T.tabr[:, 0:8], tb, TMASK, None, A.bitwise_and)
         TT(T.wr[:], "wr", T.wtr[:].indirect(T.lr[:, 0:16]), T.br[:], ["wtr", "lr", "br"], A.add)
-        for h in range(8):
-            a = slice(32 * h, 32 * h + 32)
-            emit("V", lambda: v.tensor_tensor_scan(T.key[:, a], T.wr[:, a], T.dr[:, a], -1.0, A.max, A.add), ["wr", "dr"], ["key"])
+        emit("V", lambda: v.tensor_tensor_scan(T.key[:, 0:256], T.wr[:], T.dr[:], -1.0, A.max, A.add), ["wr", "dr"], ["key"])
+        TS(T.key[:, 31:256:32], "key", T.key[:, 31:256:32], "key", float(BIG), None, A.add)
         CP(T.key[:, 256:272], "keyx", T.key[:, 0:16], "key")
         TR(T.kt[:, 0:256], "kt", T.key[:, 0:256], "key")
         TR(T.kt[:, 256:512], "kt", T.key[:, 16:272], ["key", "keyx"])
@@ -385,33 +401,38 @@ def rank_program(g, core, T, topo):
         for w in range(VUNITS, 16):
             j = 256 * (w - VUNITS)
             ACT(T.js[:, j:j + 256], "accS", T.key[:, 0:256], ["key", "kn"], AF.Sign, bias=W("kn", 0, 128, w, w + 1), accum_out=T.acc[:, w:w + 1])
-        TS(I("fi"), "fi", T.tabr[:], tb, 255, None, A.bitwise_and)
-        TS(T.prs[:], "prs", T.tabr[:, 0:8], tb, float(BIG), None, A.is_lt)
-        CP(T.tin[:, 0:16], "tin", I("fi"), "fi")
-        CP(T.tin[:, 16:32], "tin", I("fi"), "fi")
-        TT(T.prw[:], "prw", T.prs[:], T.pow[:], ["prs", "pow"], A.mult)
-        TR(T.tout[:], "tout", T.tin[:], "tin")
-        RED(T.bb[:], "bb", T.prw[:], "prw", A.add)
-        CP(T.fl[:], "fl", T.tout[:, 0:2], "tout")
-        TS(I("pf"), "pf", W("inv"), ["inv", "bb"], T.bb[:, 0:1], -0.495, A.mult, A.add)
-        TT(W("dif"), "dif", W("srf"), W("own"), ["srf", "own"], A.subtract)
-        TS(I("pg"), "pg", I("pf"), "pf", 1, None, A.bitwise_and)
-        TT(W("ph"), "ph", I("pg"), W("dif"), ["pg", "dif"], A.mult)
-        TT(W("pq"), "pq", W("ph"), W("own"), ["ph", "own"], A.add)
-        CP(T.gl[:], "gl", W("pq"), "pq")
+        if r == 0:
+            order_constants()
+        pairs = [
+            lambda: TS(I("fi"), "fi", T.tabr[:], tb, 255, None, A.bitwise_and),
+            lambda: TS(T.prs[:], "prs", T.tabr[:, 0:8], tb, float(BIG), None, A.is_lt),
+            lambda: CP(T.tin[:, 0:16], "tin", I("fi"), "fi"),
+            lambda: CP(T.tin[:, 16:32], "tin", I("fi"), "fi"),
+            lambda: TT(T.prw[:], "prw", T.prs[:], T.pow[:], ["prs", "pow"], A.mult),
+            lambda: TR(T.tout[:], "tout", T.tin[:], "tin"),
+            lambda: RED(T.bb[:], "bb", T.prw[:], "prw", A.add),
+            lambda: CP(T.fl[:], "fl", T.tout[:, 0:2], "tout"),
+            lambda: TS(I("pf"), "pf", W("inv"), ["inv", "bb"], T.bb[:, 0:1], -0.495, A.mult, A.add),
+            lambda: TT(W("dif"), "dif", W("srf"), W("own"), ["srf", "own"], A.subtract),
+            lambda: TS(I("pg"), "pg", I("pf"), "pf", 1, None, A.bitwise_and),
+            lambda: TT(W("ph"), "ph", I("pg"), W("dif"), ["pg", "dif"], A.mult),
+            lambda: TT(W("pq"), "pq", W("ph"), W("own"), ["ph", "own"], A.add),
+            lambda: CP(T.gl[:], "gl", W("pq"), "pq"),
+        ]
+        units = []
+        for w in range(VUNITS + 1):
+            if w < VUNITS:
+                units.append(lambda w=w: TS(T["jv%d" % w][:], "jv%d" % w, T.key[:, 0:256], ["key", "kn"], W("kn", 0, 128, w, w + 1), 0.0, A.add, A.is_lt))
+            if w:
+                units.append(lambda w=w - 1: RED(T.acr[:, w:w + 1], "acr", T["jv%d" % w][:], "jv%d" % w, A.add))
+        while units or pairs:
+            for todo, n in ((pairs, 2), (units, 1)):
+                for _ in range(min(n, len(todo))):
+                    todo.pop(0)()
         for t in range(4):
             ACT(T.G[:, 272 * t:272 * t + 16], "Gf%d" % t, T.G[:, 272 * t + 16:272 * t + 272].indirect(T.fl[:, 0:1]), ["G%d" % t, "fl"])
         for t in range(4):
             ACT(T.Gp[:, 256 * t:256 * t + 256], "Gp%d" % t, T.G[:, 272 * t:272 * t + 272].indirect(T.gl[:, 0:16]), ["G%d" % t, "Gf%d" % t, "gl"])
-        if r == 0:
-            order_constants()
-        for w in range(VUNITS + 1):
-            if w < VUNITS:
-                j = "jv%d" % w
-                TS(T[j][:], j, T.key[:, 0:256], ["key", "kn"], W("kn", 0, 128, w, w + 1), 0.0, A.add, A.is_lt)
-            if w:
-                j = "jv%d" % (w - 1)
-                RED(T.acr[:, w - 1:w], "acr", T[j][:], j, A.add)
         TS(T.acc[:, 0:VUNITS], "accV", T.acr[:, 0:VUNITS], "acr", -2.0, 255.0, A.mult, A.add)
         ak = ["accV", "accS"]
         TS(I("ri"), "ri", T.acc[:], ak, -0.5, 127.5, A.mult, A.add)
@@ -431,8 +452,8 @@ def rank_program(g, core, T, topo):
         QT(z, 0, 128, T.Z[:], "Z")
         need("G", toks_of("G", [z], []))
         (zc, zs), (ac, asc) = K(z, 0, 128), K(a, 0, 128)
-        g.remote_dma(ac.bitcast(dt.uint8), zc.bitcast(dt.uint8), T.sem["arr%d" % r], T.sem.sent, pid, rid, mask_c)
-        g.remote_dma(asc, zs, T.sem["arr%d" % r], T.sem.sent, pid, rid, mask_s)
+        g.remote_dma(ac.bitcast(dt.uint8), zc.bitcast(dt.uint8), T.sem["arr%d" % r], T.sem.sent, pid, rid, mask)
+        g.remote_dma(asc, zs, T.sem["arr%d" % r], T.sem.sent, pid, rid, mask)
         landed("arr%d" % r, n_in, [a, "s" + a])
         for t in range(4):
             if t < 2:
@@ -445,23 +466,25 @@ def rank_program(g, core, T, topo):
             CP(T.rl[:], "rl", I("ri"), "ri")
             emit("V", lambda: v.tensor_copy(T.opw[:].indirect(T.rl[:, 0:16]), T.vcol[:]), ["rl", "vcol"], ["opw"])
             emit("Y", lambda: g.sync.dma_start(T.op[:], T.opw[0:128:16, :]), ["opw"], ["op"], dma=True)
+        symbols(r + 1, 0)
+        if last:
+            y_columns(0)
         for b in range(4):
             MM(b, 128, "qw", 128 * b, a, 0)
             MM(4 + b, 128, "qce", 128 * b, a, 0)
             ACT(T.hr[:, 128 * b:128 * b + 128], "hr%d" % b, T["ps%d" % b][:, 0:128], "ps%d" % b, scale=0.0078125)
             TT(T.X[:, 512 + b:1024:4], "X1", T.hr[:, 128 * b:128 * b + 128], T["ps%d" % (4 + b)][:, 0:128], ["hr%d" % b, "ps%d" % (4 + b)], A.add)
-    QT("qn3", 0, 256, T.X[:], ["X0", "X1", "XS0"])
-    PICK("qp3", "qn3", T.ol[:, 0:16], "ol")
-    MM(0, 256, "qv", 0, "qp3", 0)
+    symbols(NR, 1)
+    PICK("qp3", "qn3", T.ol[:, 0:16], "ol", ["qp3"], ["na3", "nb3"])
     yc, _ = K("qp3", 0, 256)
     emit("Y", lambda: g.sync.dma_start(T.oc[:, 0:1024], yc.bitcast(dt.uint8)), ["qp3"], ["oc"], dma=True)
     for k in range(4):
         emit("Y" if k < 2 else "S", lambda: (g.sync if k < 2 else s).dma_start(T.osc[4 * k:4 * k + 4, 0:256], T.sqp[32 * k:32 * k + 4, 256 * NR:256 * NR + 256]),
              ["sqp3"], ["osc%d" % k], dma=True)
-    CP(T.ysb[:], "ysb", T.ps0[:, 0:256], "ps0")
+    y_columns(1)
     emit("Y", lambda: g.sync.dma_start(T.y[:], T.ysb[:]), ["ysb"], ["y"], dma=True)
     for k in range(nd[0]):
         g.wait_ge(T.sem["ld%d" % k], 16)
-    g.wait_ge(T.sem.sent, NR * len(eng))
+    g.wait_ge(T.sem.sent, NR * n_out)
     for k in "VSTG":
         g.wait_ge(T.sem["c" + k], count[k])

import math
from concourse.mybir import dt, AluOpType as A, AxisListType, ActivationFunctionType as AF

NR = 3
VUNITS = 4
BIG = 1 << 20
TMASK = 0x7FF00
INTS = ["oi", "oj", "ok1", "ni", "nj", "nk", "fi", "pf", "pg", "ri", "rx"]
FLTS = ["s1", "sn", "inv", "dif", "own", "ph", "pq", "ka", "kb", "ry", "rz", "of", "srf", "kn"]

SCRATCH = {}


def _b(name, n, d="float32"):
    SCRATCH[name] = ("sbuf", [128, n], d)


for _n, _k, _d in (
        ("xs", 1024, "bfloat16"), ("us", 512, "bfloat16"), ("vs", 512, "bfloat16"),
        ("one", 128, "bfloat16"), ("zer", 528, "bfloat16"), ("dy", 128, "bfloat16"), ("dy0", 128, "bfloat16"), ("dy1", 128, "bfloat16"),
        ("dya", 128, "bfloat16"), ("dyb", 128, "bfloat16"), ("dyc", 128, "bfloat16"),
        ("idn", 128, "bfloat16"), ("prm", 128, "bfloat16"),
        ("cl", 2560, "bfloat16"), ("ce", 528, "bfloat16"), ("cg", 528, "bfloat16"),
        ("pI", 1, "int32"), ("pi8", 1, "int32"), ("pi4", 1, "int32"), ("pi16", 1, "int32"), ("pih", 1, "int32"),
        ("mk", 4, "float32"), ("cm", 2, "float32"), ("c8", 2, "float32"), ("cf", 8, "float32"),
        ("io8", 8, "float32"), ("dT", 16, "float32"), ("pen", 8, "float32"), ("pwf", 8, "float32"), ("pow", 8, "int32"),
        ("bp", 128, "float32"), ("br", 256, "float32"),
        ("ti", 256, "int32"), ("tj", 256, "int32"), ("vrow", 256, "bfloat16"), ("vcol", 256, "float32"),
        ("ol", 16, "uint16"), ("nl", 16, "uint16"),
        ("sb", 48, "float32"), ("mt", 512, "bfloat16"),
        ("l0", 8, "uint16"), ("l1", 8, "uint16"), ("l2", 8, "uint16"), ("lr", 16, "uint16"),
        ("da", 128, "float32"), ("db", 128, "float32"), ("dc", 128, "float32"), ("dr", 256, "float32"),
        ("wp", 128, "float32"), ("wr", 256, "float32"), ("tp", 128, "float32"), ("mm", 128, "float32"), ("mv", 1, "float32"),
        ("rep", 32, "float32"), ("trp", 32, "float32"), ("tab0", 16, "int32"), ("tab1", 16, "int32"), ("tabr", 16, "int32"),
        ("wt", 8, "int32"), ("wtr", 16, "int32"), ("tin", 32, "float32"), ("tout", 32, "float32"),
        ("fl", 2, "uint16"), ("prs", 8, "float32"), ("prw", 8, "float32"), ("bb", 1, "float32"), ("gl", 16, "uint16"),
        ("key", 272, "float32"), ("kt", 512, "float32"), ("acc", 16, "float32"), ("acr", 16, "float32"),
        ("pl", 16, "uint16"), ("rl", 16, "uint16"),
        ("win", 512, "bfloat16"), ("wtt", 512, "bfloat16"), ("ou", 16, "uint16"), ("opw", 256, "float32"),
        ("F", 1024, "bfloat16"), ("G", 1088, "bfloat16"), ("Gp", 1024, "bfloat16"), ("gz", 512, "bfloat16"), ("Z", 512, "bfloat16"),
        ("X", 1024, "bfloat16"), ("hr", 512, "float32"), ("ysb", 256, "float32")):
    _b(_n, _k, _d)
_b("js", 256 * (16 - VUNITS), "bfloat16")
for _k in range(VUNITS):
    _b("jv%d" % _k, 256, "bfloat16")
_b("ints", 16 * len(INTS), "int32")
_b("flts", 16 * len(FLTS), "float32")
for _n, _k in (("qx", 256), ("qn", 1024), ("qp", 1024), ("qu", 128), ("qv", 128), ("qw", 512), ("qc", 1664), ("qm", 128),
               ("qz", 128 * NR), ("qa", 128 * NR)):
    _b(_n, _k, "float8_e4m3fn_x4")
    _b("s" + _n, _k, "uint8")
for _k in range(8):
    SCRATCH["ps%d" % _k] = ("psum", [128, 512], "float32")
SEMAPHORES = ["cV", "cS", "cT", "cG", "sent"] + ["arr%d" % k for k in range(NR)] + ["ld%d" % k for k in range(16)]


def recorder(g, T):
    eng = {"V": g.vector, "S": g.scalar, "T": g.tensor, "G": g, "Y": g.sync}
    count = {"V": 0, "S": 0, "T": 0, "G": 0}
    known = {q: {} for q in eng}
    writer, readers = {}, {}
    nd = [0]

    def need(q, toks):
        todo = {}
        for (sem, val, own, snap) in toks:
            if known[q].get(sem, 0) < val and todo.get(sem, (0, None))[0] < val:
                todo[sem] = (val, snap)
        for sem in list(todo):
            if any(s != sem and todo[s][1].get(sem, 0) >= todo[sem][0] for s in todo):
                continue
            eng[q].wait_ge(T.sem[sem], todo[sem][0])
        for sem, (val, snap) in todo.items():
            for k, v in list(snap.items()) + [(sem, val)]:
                if known[q].get(k, 0) < v:
                    known[q][k] = v

    def toks_of(q, reads, writes):
        t = []
        for r in reads:
            if r in writer:
                t.append(writer[r])
            if r[:2] == "ps":
                t += [x for x in readers.get(r, []) if x[2] != q]
        for w in writes:
            t += readers.get(w, [])
            if w in writer and (writer[w][2] != q or readers.get(w)):
                t.append(writer[w])
        return t

    def note(tok, reads, writes):
        for w in writes:
            writer[w] = tok
            readers[w] = []
        for r in reads:
            if r not in writes:
                readers.setdefault(r, []).append(tok)

    def emit(q, make, reads, writes, dma=False):
        need(q, toks_of(q, reads, writes))
        ins = make()
        if dma:
            sem = "ld%d" % nd[0]
            nd[0] += 1
            ins.then_inc(T.sem[sem], 16)
            tok = (sem, 16, "D" + sem, dict(known[q]))
        else:
            sem = "c" + q
            count[q] += 1
            ins.then_inc(T.sem[sem], 1)
            tok = (sem, count[q], q, dict(known[q]))
        note(tok, reads, writes)
        return tok

    def landed(sem, val, writes):
        note((sem, val, "R" + sem, {}), [], writes)

    return emit, need, toks_of, landed, count, nd


def rank_program(g, core, T, topo):
    rank = T.rank_of(core)
    if rank is None:
        return
    nxt = T.cores[(rank + 1) % len(T.cores)]
    prv = T.cores[(rank - 1) % len(T.cores)]
    emit, need, toks_of, landed, count, nd = recorder(g, T)
    v, s = g.vector, g.scalar

    def I(n):
        k = 16 * INTS.index(n)
        return T.ints[:, k:k + 16]

    def W(n, p0=0, p1=128, a=0, b=16):
        k = 16 * FLTS.index(n)
        return T.flts[p0:p1, k + a:k + b]

    place = {"qcl": ("qc", 0), "qcr": ("qc", 384), "qce": ("qc", 640), "qcg": ("qc", 1152)}
    for k in range(NR + 1):
        place["qn%d" % k] = ("qn", 256 * k)
        place["na%d" % k] = ("qn", 256 * k)
        place["nb%d" % k] = ("qn", 256 * k + 128)
        place["qp%d" % k] = ("qp", 256 * k)
        place["qz%d" % k] = ("qz", 128 * k)
        place["qa%d" % k] = ("qa", 128 * k)

    def K(n, a, b):
        q, o = place.get(n, (n, 0))
        return T[q][:, o + a:o + b], T["s" + q][:, o + a:o + b]

    def pt(n):
        return n if isinstance(n, (list, tuple)) else [n]

    def TS(o, ok, i, ik, s1, s2, o0, o1=None):
        if o1 is None:
            return emit("V", lambda: v.tensor_scalar(o, i, s1, None, o0), pt(ik), pt(ok))
        return emit("V", lambda: v.tensor_scalar(o, i, s1, s2, o0, o1), pt(ik), pt(ok))

    def TT(o, ok, a, b, ik, op):
        return emit("V", lambda: v.tensor_tensor(o, a, b, op), pt(ik), pt(ok))

    def CP(o, ok, i, ik):
        return emit("V", lambda: v.tensor_copy(o, i), pt(ik), pt(ok))

    def ACT(o, ok, i, ik, f=AF.Copy, **kw):
        return emit("S", lambda: s.activation(o, i, f, **kw), pt(ik), pt(ok))

    def TR(o, ok, i, ik):
        return emit("V", lambda: v.transpose(o, i), pt(ik), pt(ok))

    def RED(o, ok, i, ik, op):
        return emit("V", lambda: v.tensor_reduce(o, i, AxisListType.X, op), pt(ik), pt(ok))

    def FILL(ap, ok, c):
        return emit("V", lambda: v.memset(ap, c), [], pt(ok))

    def QT(q, a, b, i, ik):
        return emit("V", lambda: v.quantize_mx(*K(q, a, b), i), pt(ik), [q, "s" + q])

    def MM(bank, n, w, wa, m, ma):
        (wt, ws), (mt, ms) = K(w, wa, wa + 128), K(m, ma, ma + n)
        o = T["ps%d" % bank][:, 0:n]
        return emit("T", lambda: g.tensor.matmul_mx(o, wt, ws, mt, ms, True, True), [w, "s" + w, m, "s" + m], ["ps%d" % bank])

    def PICK(o, i, lst, lk, ok, ik):
        (oc, osc), (ic, isc) = K(o, 0, 256), K(i, 0, 256)
        emit("V", lambda: v.tensor_copy(oc.bitcast(dt.uint32), ic.bitcast(dt.uint32).indirect(lst)), ik + [lk], ok)
        emit("S", lambda: s.activation(osc, isc.indirect(lst), AF.Copy), ["s" + k for k in ik] + [lk], ["s" + k for k in ok])

    def IOTA(ap, ok, pat, base, cm, f=True):
        if f:
            return emit("G", lambda: g.iota(ap, pat, base, cm, allow_small_or_imprecise_dtypes=True), [], pt(ok))
        return emit("G", lambda: g.iota(ap, pat, base, cm), [], pt(ok))

    def AFF(o, ok, i, ik, pat, op, base, cm):
        return emit("G", lambda: g.affine_select(o, i, pat, op, 0.0, base, cm), pt(ik), pt(ok))

    emit("Y", lambda: g.sync.dma_start(T.xs[:], T.x[:]), [], ["xs"], dma=True)
    emit("S", lambda: s.dma_start(T.us[:], T.u[:]), [], ["us"], dma=True)
    emit("Y", lambda: g.sync.dma_start(T.qw[:, 0:512].bitcast(dt.uint8), T.wc[:, 0:2048]), [], ["qw"], dma=True)
    emit("Y", lambda: g.sync.dma_start(T.sqw[:, 0:512], T.ws[:, 0:512]), [], ["sqw"], dma=True)
    emit("Y", lambda: g.sync.dma_start(T.vs[:], T.v[:]), [], ["vs"], dma=True)

    FILL(T.one[:], "one", 1.0)
    IOTA(T.pI[:], "pI", [[0, 1]], 0, 1, False)
    IOTA(T.io8[:], "io8", [[1, 8]], 0, 0)
    IOTA(I("ni"), "ni", [[16, 16]], 0, 1, False)
    AFF(T.dyb[:], "dyb", T.one[:], "one", [[0, 8], [-8, 16]], A.is_ge, 0, 1)
    AFF(T.dy0[:], "dy0", T.dyb[:], "dyb", [[0, 8], [8, 16]], A.is_ge, 3, -1)
    AFF(T.dyc[:], "dyc", T.one[:], "one", [[0, 8], [-8, 16]], A.is_ge, -4, 1)
    AFF(T.dy1[:], "dy1", T.dyc[:], "dyc", [[0, 8], [8, 16]], A.is_ge, 7, -1)
    AFF(T.dya[:], "dya", T.one[:], "one", [[0, 4], [-4, 2], [-8, 16]], A.is_ge, 0, 1)
    AFF(T.dy[:], "dy", T.dya[:], "dya", [[0, 4], [4, 2], [8, 16]], A.is_ge, 3, -1)
    IOTA(T.bp[:], "bp0", [[1, 128]], -1, 0)
    AFF(T.idn[:], "idn", T.one[:], "one", [[-1, 128]], A.is_equal, 0, 1)
    AFF(T.prm[:], "prm0", T.one[:], "one", [[-16, 4], [0, 2], [-1, 16]], A.is_equal, 0, 1)
    AFF(T.prm[:, 0:16], "prm", T.one[:, 0:16], ["one", "prm0"], [[-1, 16]], A.is_equal, -112, 1)
    IOTA(T.br[:], "br", [[1, 256]], -1, 0)
    IOTA(T.ti[:], "ti", [[16, 2], [32, 8], [1, 16]], 0, 0, False)

    FILL(T.zer[:], "zer", 0.0)
    ACT(T.cl[:, 1536:2048], "cl0S", T.zer[:, 0:512], "zer")
    ACT(T.cl[:, 2048:2560], "cl0S", T.zer[:, 0:512], "zer")
    ACT(T.mt[:], "mt0", T.zer[:, 0:512], "zer")
    ACT(T.pwf[:], "pwf", T.io8[:], "io8", AF.Exp, scale=math.log(2.0))
    FILL(T.cl[:, 0:1536], "cl0", 0.0)
    TS(T.pi16[:], "pi16", T.pI[:], "pI", 15, None, A.bitwise_and)
    TS(T.pi8[:], "pi8", T.pI[:], "pI", 7, None, A.bitwise_and)
    TS(T.pi4[:], "pi4", T.pI[:], "pI", 3, None, A.bitwise_and)
    TS(T.pih[:], "pih", T.pI[:], "pI", 4, 1, A.arith_shift_right, A.bitwise_and)
    TS(T.cf[:, 5:6], "cf5", T.pI[:], "pI", 1.0, None, A.mult)
    TS(T.cf[:, 4:5], "cf4", T.pi16[:], "pi16", 1.0, None, A.mult)
    TT(T.cf[:, 3:4], "cf3", T.cf[:, 4:5], T.cf[:, 5:6], ["cf4", "cf5"], A.subtract)
    TS(I("nj"), "nj", I("ni"), ["ni", "cf3"], T.cf[:, 3:4], None, A.add)
    TS(I("nk"), "nk", I("nj"), "nj", 7, None, A.bitwise_and)
    TS(I("ok1"), "ok1", I("nj"), "nj", 3, None, A.arith_shift_right)
    TS(I("oi"), "oi", I("nk"), "nk", 32.0, None, A.mult)
    TT(I("nk"), "nk", I("oi"), I("ok1"), ["oi", "ok1"], A.add)
    CP(T.nl[:], "nl", I("nk"), "nk")
    for h in range(4):
        TS(T.mk[:, h:h + 1], "mk", T.pi4[:], "pi4", float(h), None, A.is_equal)
    TS(T.c8[:, 0:1], "c80", T.pI[:], "pI", 16.0, 8.0, A.is_lt, A.mult)
    TS(T.c8[:, 1:2], "c81", T.pI[:], "pI", 16.0, -10.0, A.is_lt, A.mult)
    for y, nm in ((0, "dy0"), (1, "dy1")):
        for G in range(8):
            o = 1536 + 512 * y + 64 * G + G % 4
            ACT(T.cl[:, o:o + 61:4], "clS", T[nm][:, 16 * G:16 * G + 16], [nm, "cl0S"])

    QT("qx", 0, 256, T.xs[:], "xs")
    QT("qu", 0, 128, T.us[:], "us")
    PICK("qn0", "qx", T.nl[:, 0:16], "nl", ["na0", "nb0"], ["qx"])
    ACT(T.cg[:], "cg0", T.zer[:], "zer")
    ACT(T.ce[:], "ce0", T.zer[:], "zer")
    ACT(T.win[:], "win", T.zer[:, 0:512], "zer")
    CP(T.cl[:, 0:512:4], "clV", T.dy[:], ["dy", "cl0"])
    CP(T.cl[:, 513:1024:4], "clV", T.dy[:], "dy")
    for k in range(4):
        o = 1024 + 128 * k + 2 + k % 2
        CP(T.cl[:, o:o + 125:4], "clV", T.dy[:, 32 * k:32 * k + 32], "dy")
    QT("qcl", 0, 384, T.cl[:, 0:1536], "clV")
    QT("qcr", 0, 256, T.cl[:, 1536:2560], "clS")

    def path_constants():
        TS(T.dT[:, 0:8], "dT", T.io8[:], "io8", 256.0, 257.0, A.mult, A.add)
        TS(T.dT[:, 8:16], "dT", T.io8[:], "io8", 256.0, 257.0, A.mult, A.add)
        TS(T.cf[:, 2:3], "cf2", T.pi8[:], "pi8", 1.0, None, A.mult)
        TS(T.pen[:], "pen", T.io8[:], ["io8", "cf2"], T.cf[:, 2:3], float(BIG), A.not_equal, A.mult)
        TS(T.cf[:, 1:2], "cf1", T.pih[:], "pih", 128.0, None, A.mult)
        TS(T.bp[:], "bp", T.bp[:], ["bp0", "cf1"], T.cf[:, 1:2], None, A.add)
        emit("V", lambda: v.memset(T.wtr[:], 0), [], ["wtr"])
        CP(T.pow[:], "pow", T.pwf[:], "pwf")

    def key_constants():
        TS(T.cm[:, 0:1], "cm", T.pih[:], "pih", 0.0, -1.0, A.is_equal, A.mult)
        TS(T.cm[:, 1:2], "cm", T.pih[:], "pih", -1.0, None, A.mult)
        TS(W("own"), "own", I("nj"), "nj", 16.0, None, A.add)

    def order_constants():
        TS(T.cf[:, 0:1], "cf0", T.pih[:], "pih", 16.0, 255.0, A.mult, A.add)
        TS(T.cf[:, 6:7], "cf6", T.pih[:], "pih", 16.0, None, A.mult)
        TS(T.tj[:], "tj", T.ti[:], ["ti", "cf6"], T.cf[:, 6:7], None, A.add)
        TS(T.ti[:], "ti", T.tj[:], "tj", 255, None, A.bitwise_and)
        CP(T.vrow[:], "vrow", T.ti[:], "ti")

    def column_constants():
        CP(T.vcol[:], "vcol", T.ti[:], "ti")
        TS(I("oi"), "oi", I("nj"), "nj", 31, None, A.bitwise_and)
        TS(I("oj"), "oj", I("nj"), "nj", 5, None, A.arith_shift_right)
        TS(I("ok1"), "ok1", I("oi"), "oi", 8.0, None, A.mult)
        TT(I("oi"), "oi", I("ok1"), I("oj"), ["ok1", "oj"], A.add)
        CP(T.ol[:], "ol", I("oi"), "oi")
        QT("qv", 0, 128, T.vs[:], "vs")

    rid, pid, _ = topo.addr(nxt)
    mask = topo.mask(core, nxt)
    n_out, n_in = 2 * len(topo.engines(core, nxt)), 2 * len(topo.engines(prv, core))

    def symbols(k, hf):
        q = ("na%d", "nb%d")[hf] % k
        if k:
            QT(q, 0, 128, T.X[:, 512 * hf:512 * hf + 512], [["X0", "XS0"], ["X1"]][hf])
        if k == NR:
            MM(hf, 128, "qv", 0, q, 0)
            return
        MM(hf, 128, q, 0, "qu", 0)
        a, b = 8 * hf, 8 * hf + 8
        for i in range(3):
            TS(T.sb[:, 16 * i + a:16 * i + b], "sb%d" % hf, T["ps%d" % hf][:, i:128:16], "ps%d" % hf, 0.0, float(4 >> i), A.is_gt, A.mult)
        TT(W("s1", 0, 128, a, b), "s1%d" % hf, T.sb[:, a:b], T.sb[:, 16 + a:16 + b], "sb%d" % hf, A.add)
        TT(W("sn", 0, 128, a, b), "sn%d" % hf, W("s1", 0, 128, a, b), T.sb[:, 32 + a:32 + b], ["s1%d" % hf, "sb%d" % hf], A.add)
        for h in range(4):
            o, sn = T.mt[:, 16 * h + a:16 * h + b], W("sn", 0, 128, a, b)
            if h < 2:
                TS(o, "mt%dv" % hf, sn, ["sn%d" % hf, "mk", "mt0"], T.mk[:, h:h + 1], None, A.mult)
            else:
                ACT(o, "mt%ds" % hf, sn, ["sn%d" % hf, "mk", "mt0"], scale=T.mk[:, h:h + 1])

    def y_columns(hf):
        for h in range(8):
            CP(T.ysb[:, 32 * h + 16 * hf:32 * h + 16 * hf + 16], "ysb", T["ps%d" % hf][:, h:128:8], "ps%d" % hf)

    def level(w, d, lst):
        for h in range(4):
            a = slice(32 * h, 32 * h + 32)
            emit("V", lambda: v.tensor_tensor_scan(T.tp[:, a], T[w][:, a], T[d][:, a], -1.0, A.max, A.add), [w, d], ["tp"])
        TT(T.mm[:], "mm", T.pen[:].indirect(T[lst][:, 0:8]), T.tp[:], ["pen", lst, "tp"], A.max)
        RED(T.mv[:], "mv", T.mm[:], "mm", A.min)
        TS(T.rep[:], "rep", T.zer[:, 0:32], ["zer", "mv"], T.mv[:, 0:1], None, A.add)
        TR(T.trp[:], "trp", T.rep[:], "rep")

    def waits(k, lst):
        tab = "tab%d" % k
        TT(T[tab][:], tab, T.trp[:, 0:16], T.trp[:, 16:32], "trp", A.min)
        TS(T.wt[:], "wt", T[tab][:, 0:8], tab, TMASK, None, A.bitwise_and)
        CP(T.tabr[32 * k:32 * k + 32, :], "tabr%d" % k, T[tab][32 * k:32 * k + 32, :], tab)
        TT(T.wp[:], "wp", T.wt[:].indirect(T[lst][:, 0:8]), T.bp[:], ["wt", lst, "bp"], A.add)

    for r in range(NR):
        last = r == NR - 1
        if r == 0:
            symbols(0, 0)
        symbols(r, 1)
        QT("qm", 0, 128, T.mt[:], ["mt0v", "mt0s", "mt1v", "mt1s"])
        for k in range(3):
            MM(2 + k, 128, "qcl", 128 * k, "qm", 0)
        for k in range(2):
            MM(5 + k, 128, "qcr", 128 * k, "qm", 0)
        if r == 0:
            path_constants()
            fq = "qx"
            ACT(T.cg[:, 3:512:4], "cg", T.prm[:], ["prm", "cg0"])
            ACT(T.ce[:, 3:512:4], "ce", T.idn[:], ["idn", "ce0"])
        else:
            fq = "qp%d" % r
            PICK(fq, "qn%d" % r, T.ol[:, 0:16], "ol", [fq], ["na%d" % r, "nb%d" % r])
        CP(T.l0[:], "l0", T.ps2[:, 0:16:2], "ps2")
        CP(T.da[:], "da", T.dT[:, 0:8].indirect(T.l0[:, 0:8]), ["dT", "l0"])
        CP(T.l1[:], "l1", T.ps3[:, 0:16:2], "ps3")
        ACT(T.db[:], "db", T.dT[:, 0:8].indirect(T.l1[:, 0:8]), ["dT", "l1"])
        for y in range(2):
            for hf in range(2):
                ACT(W("srf", 64 * hf, 64 * hf + 64, 8 * y, 8 * y + 8), "srf", T["ps%d" % (5 + y)][64 * hf:64 * hf + 64, hf:16:2], ["ps%d" % (5 + y), "c80"],
                    AF.Identity, bias=T.c8[64 * hf:64 * hf + 64, 0:1])
        level("bp", "da", "l0")
        waits(0, "l1")
        CP(T.l2[:], "l2", T.ps4[:, 0:16:2], "ps4")
        ACT(T.dc[:], "dc", T.dT[:, 0:8].indirect(T.l2[:, 0:8]), ["dT", "l2"])
        CP(T.lr[:], "lr", W("srf"), "srf")
        ACT(T.dr[:], "dr", T.dT[:].indirect(T.lr[:, 0:16]), ["dT", "lr"])
        ACT(T.dr[:, 31:256:32], "dr", T.dr[:, 31:256:32], "dr", AF.Identity, bias=-float(BIG))
        ACT(W("inv"), "inv", W("srf"), ["srf", "c81"], AF.Exp, bias=T.c8[:, 1:2], scale=-math.log(2.0))
        level("wp", "db", "l1")
        waits(1, "l2")
        if r == 0:
            for b in range(4):
                QT("qcg", 128 * b, 128 * b + 128, T.cg[:, 3 - b:515 - b], "cg")
            for b in range(4):
                QT("qce", 128 * b, 128 * b + 128, T.ce[:, 3 - b:515 - b], "ce")
        for j in range(8):
            b, src, bk = j % 4, ("qcg", "qce")[j // 4], (7, 0, 1, 2, 3, 4, 5, 6)[j]
            MM(bk, 256, src, 128 * b, fq, 0)
            if j < 4:
                ACT(T.G[:, 272 * b + 16:272 * b + 272], "G%d" % b, T["ps%d" % bk][:, 0:256], "ps%d" % bk, scale=0.5)
            else:
                ACT(T.F[:, 256 * b:256 * b + 256], "F%d" % b, T["ps%d" % bk][:, 0:256], "ps%d" % bk, scale=0.5)
        level("wp", "dc", "l2")
        TT(T.tabr[64:128, :], "tabr2", T.trp[64:128, 0:16], T.trp[64:128, 16:32], "trp", A.min)
        tb = ["tabr0", "tabr1", "tabr2"]
        TS(T.wtr[:, 0:8], "wtr", T.tabr[:, 0:8], tb, TMASK, None, A.bitwise_and)
        TT(T.wr[:], "wr", T.wtr[:].indirect(T.lr[:, 0:16]), T.br[:], ["wtr", "lr", "br"], A.add)
        emit("V", lambda: v.tensor_tensor_scan(T.key[:, 0:256], T.wr[:], T.dr[:], -1.0, A.max, A.add), ["wr", "dr"], ["key"])
        TS(T.key[:, 31:256:32], "key", T.key[:, 31:256:32], "key", float(BIG), None, A.add)
        CP(T.key[:, 256:272], "keyx", T.key[:, 0:16], "key")
        TR(T.kt[:, 0:256], "kt", T.key[:, 0:256], "key")
        TR(T.kt[:, 256:512], "kt", T.key[:, 16:272], ["key", "keyx"])
        if r == 0:
            key_constants()
        TS(W("ka"), "ka", T.kt[:, 0:512:32], ["kt", "cm"], T.cm[:, 0:1], None, A.mult)
        TS(W("kb"), "kb", T.kt[:, 16:512:32], ["kt", "cm"], T.cm[:, 1:2], None, A.mult)
        TT(W("kn"), "kn", W("ka"), W("kb"), ["ka", "kb"], A.add)
        for w in range(VUNITS, 16):
            j = 256 * (w - VUNITS)
            ACT(T.js[:, j:j + 256], "accS", T.key[:, 0:256], ["key", "kn"], AF.Sign, bias=W("kn", 0, 128, w, w + 1), accum_out=T.acc[:, w:w + 1])
        if r == 0:
            order_constants()
        pairs = [
            lambda: TS(I("fi"), "fi", T.tabr[:], tb, 255, None, A.bitwise_and),
            lambda: TS(T.prs[:], "prs", T.tabr[:, 0:8], tb, float(BIG), None, A.is_lt),
            lambda: CP(T.tin[:, 0:16], "tin", I("fi"), "fi"),
            lambda: CP(T.tin[:, 16:32], "tin", I("fi"), "fi"),
            lambda: TT(T.prw[:], "prw", T.prs[:], T.pow[:], ["prs", "pow"], A.mult),
            lambda: TR(T.tout[:], "tout", T.tin[:], "tin"),
            lambda: RED(T.bb[:], "bb", T.prw[:], "prw", A.add),
            lambda: CP(T.fl[:], "fl", T.tout[:, 0:2], "tout"),
            lambda: TS(I("pf"), "pf", W("inv"), ["inv", "bb"], T.bb[:, 0:1], -0.495, A.mult, A.add),
            lambda: TT(W("dif"), "dif", W("srf"), W("own"), ["srf", "own"], A.subtract),
            lambda: TS(I("pg"), "pg", I("pf"), "pf", 1, None, A.bitwise_and),
            lambda: TT(W("ph"), "ph", I("pg"), W("dif"), ["pg", "dif"], A.mult),
            lambda: TT(W("pq"), "pq", W("ph"), W("own"), ["ph", "own"], A.add),
            lambda: CP(T.gl[:], "gl", W("pq"), "pq"),
        ]
        units = []
        for w in range(VUNITS + 1):
            if w < VUNITS:
                units.append(lambda w=w: TS(T["jv%d" % w][:], "jv%d" % w, T.key[:, 0:256], ["key", "kn"], W("kn", 0, 128, w, w + 1), 0.0, A.add, A.is_lt))
            if w:
                units.append(lambda w=w - 1: RED(T.acr[:, w:w + 1], "acr", T["jv%d" % w][:], "jv%d" % w, A.add))
        while units or pairs:
            for todo, n in ((pairs, 2), (units, 1)):
                for _ in range(min(n, len(todo))):
                    todo.pop(0)()
        for t in range(4):
            ACT(T.G[:, 272 * t:272 * t + 16], "Gf%d" % t, T.G[:, 272 * t + 16:272 * t + 272].indirect(T.fl[:, 0:1]), ["G%d" % t, "fl"])
        for t in range(4):
            ACT(T.Gp[:, 256 * t:256 * t + 256], "Gp%d" % t, T.G[:, 272 * t:272 * t + 272].indirect(T.gl[:, 0:16]), ["G%d" % t, "Gf%d" % t, "gl"])
        TS(T.acc[:, 0:VUNITS], "accV", T.acr[:, 0:VUNITS], "acr", -2.0, 255.0, A.mult, A.add)
        ak = ["accV", "accS"]
        TS(I("ri"), "ri", T.acc[:], ak, -0.5, 127.5, A.mult, A.add)
        TS(W("ry"), "ry", T.acc[:], ak + ["cf0"], -1.0, T.cf[:, 0:1], A.mult, A.add)
        TS(I("rx"), "rx", I("ri"), "ri", 15, None, A.bitwise_and)
        TT(W("rz"), "rz", W("ry"), I("rx"), ["ry", "rx"], A.subtract)
        CP(T.pl[:], "pl", W("rz"), "rz")
        emit("V", lambda: v.tensor_copy(T.win[:].indirect(T.pl[:, 0:16]), T.vrow[:]), ["pl", "vrow", "win"], ["win"])
        TR(T.wtt[:], "wtt", T.win[:], "win")
        TT(W("of"), "of", T.wtt[:, 0:512:32], T.wtt[:, 16:512:32], "wtt", A.add)
        CP(T.ou[:], "ou", W("of"), "of")
        for t in range(4):
            ACT(T.gz[:, 128 * t:128 * t + 128], "gz%d" % t, T.Gp[:, 256 * t:256 * t + 256].indirect(T.ou[:, 0:8]), ["Gp%d" % t, "ou"])
        for t in range(4):
            TT(T.Z[:, t:512:4], "Z", T.F[:, 256 * t:256 * t + 256].indirect(T.ou[:, 0:8]), T.gz[:, 128 * t:128 * t + 128], ["F%d" % t, "ou", "gz%d" % t], A.add)
        z, a = "qz%d" % r, "qa%d" % r
        QT(z, 0, 128, T.Z[:], "Z")
        need("G", toks_of("G", [z], []))
        (zc, zs), (ac, asc) = K(z, 0, 128), K(a, 0, 128)
        g.remote_dma(ac.bitcast(dt.uint8), zc.bitcast(dt.uint8), T.sem["arr%d" % r], T.sem.sent, pid, rid, mask)
        g.remote_dma(asc, zs, T.sem["arr%d" % r], T.sem.sent, pid, rid, mask)
        landed("arr%d" % r, n_in, [a, "s" + a])
        for t in range(4):
            if t < 2:
                TS(T.X[:, t:512:4], "X0", T.F[:, 256 * t:256 * t + 256].indirect(T.ou[:, 8:16]), ["F%d" % t, "ou"], 2.0, None, A.mult)
            else:
                ACT(T.X[:, t:512:4], "XS0", T.F[:, 256 * t:256 * t + 256].indirect(T.ou[:, 8:16]), ["F%d" % t, "ou"], scale=2.0)
        if r == 0:
            column_constants()
        if last:
            CP(T.rl[:], "rl", I("ri"), "ri")
            emit("V", lambda: v.tensor_copy(T.opw[:].indirect(T.rl[:, 0:16]), T.vcol[:]), ["rl", "vcol"], ["opw"])
            emit("Y", lambda: g.sync.dma_start(T.op[:], T.opw[0:128:16, :]), ["opw"], ["op"], dma=True)
        symbols(r + 1, 0)
        if last:
            y_columns(0)
        for b in range(4):
            MM(b, 128, "qw", 128 * b, a, 0)
            MM(4 + b, 128, "qce", 128 * b, a, 0)
            ACT(T.hr[:, 128 * b:128 * b + 128], "hr%d" % b, T["ps%d" % b][:, 0:128], "ps%d" % b, scale=0.0078125)
            TT(T.X[:, 512 + b:1024:4], "X1", T.hr[:, 128 * b:128 * b + 128], T["ps%d" % (4 + b)][:, 0:128], ["hr%d" % b, "ps%d" % (4 + b)], A.add)
    symbols(NR, 1)
    PICK("qp3", "qn3", T.ol[:, 0:16], "ol", ["qp3"], ["na3", "nb3"])
    yc, _ = K("qp3", 0, 256)
    emit("Y", lambda: g.sync.dma_start(T.oc[:, 0:1024], yc.bitcast(dt.uint8)), ["qp3"], ["oc"], dma=True)
    for k in range(4):
        emit("Y" if k < 2 else "S", lambda: (g.sync if k < 2 else s).dma_start(T.osc[4 * k:4 * k + 4, 0:256], T.sqp[32 * k:32 * k + 4, 256 * NR:256 * NR + 256]),
             ["sqp3"], ["osc%d" % k], dma=True)
    y_columns(1)
    emit("Y", lambda: g.sync.dma_start(T.y[:], T.ysb[:]), ["ysb"], ["y"], dma=True)
    for k in range(nd[0]):
        g.wait_ge(T.sem["ld%d" % k], 16)
    g.wait_ge(T.sem.sent, NR * n_out)
    for k in "VSTG":
        g.wait_ge(T.sem["c" + k], count[k])
